import numpy as np, ml_dtypes
CORES = [13,21,141,149]
N = 4
BF = ml_dtypes.bfloat16
W, H0, L, RO, Q = 2048, 768, 256, 2, 4
def base(rng):
    price = rng.integers(0, 101, (N, 8, 1, W)) + rng.integers(0, 28, (N, 8, 16, W))
    packs = rng.integers(0, W, (N, 8, 16, H0)); prev = rng.integers(0, H0, (N, 8, H0)); lots = rng.integers(0, W, (N, 8, 16, L))
    lots[:, :, 0, ::4] = lots[:1, :, 0, ::4]
    o = np.stack([rng.permutation(np.array([5, 20, 35, 50, 60, 70, 80, 90])) for q in range(N)])
    slack = o[:, :, None, None] + rng.integers(0, 9, (N, 8, 16, RO))
    return price, packs, prev, lots, rng.integers(1, 8, (N, 8, 16)), rng.integers(0, 16, (N, 8, 16)), slack
def pack(price, packs, prev, lots, inc, wt, slack):
    c = lambda a, n: np.ascontiguousarray(np.reshape(a, (N, 128, n))).astype(np.int32)
    return {"price": np.ascontiguousarray(price.reshape(N, 128, W)).astype(np.float32).astype(BF), "packs": c(packs, H0), "prev": np.ascontiguousarray(prev).astype(np.int32),
            "lots": c(lots, L), "inc": c(inc, 1), "wt": c(wt, 1), "slack": c(slack, RO)}
def edge(rng, hi, *s):
    return np.where(rng.random(s) < 0.2, rng.integers(0, hi + 1, s), hi * rng.integers(0, 2, s))
def setup_inputs(rng):
    return pack(*base(rng))
def setup_inputs_spread(rng):
    price, packs, prev, lots, inc, wt, slack = base(rng)
    price = np.minimum((np.exp2(7.65 * rng.random((N, 8, 1, W))) * rng.random((N, 8, 16, W))).astype(np.int64), 200)
    packs = np.minimum((W * rng.random((N, 8, 16, H0)) ** 3).astype(np.int64), W - 1)
    lots = W - 1 - np.minimum((W * rng.random((N, 8, 16, L)) ** 2).astype(np.int64), W - 1)
    prev = np.minimum((H0 * rng.random((N, 8, H0)) ** 2).astype(np.int64), H0 - 1)
    slack = np.minimum(np.exp2(8 * rng.random((N, 8, 1, 1)) * rng.random((N, 8, 16, RO))).astype(np.int64) - 1, 255)
    return pack(price, packs, prev, lots, inc, wt, slack)
def setup_inputs_ends(rng):
    hi = np.where(np.arange(8) == 6, 127, 200)[None, :, None, None]
    k = rng.integers(0, 3, (N, 8, 1, W)); price = hi * np.where(k == 2, rng.integers(0, 2, (N, 8, 16, W)), k)
    price[..., 0] = 0; price[..., W - 1] = hi[..., 0]
    price[:, 2:4, :, 0] = 200; price[:, 2:4, :, W - 1] = 0; price[:, 5, 9:, W - 1] = 0
    packs = edge(rng, W - 1, N, 8, 16, H0); prev = edge(rng, H0 - 1, N, 8, H0); lots = edge(rng, W - 1, N, 8, 16, L)
    inc = 1 + 6 * rng.integers(0, 2, (N, 8, 16)); inc[:, 7] = 7; inc[:, 6, 0] = 1
    o = np.argsort(rng.random((N, 8, 16)), axis=2)
    slack = np.repeat((255 * (o >= np.array([16, 9, 16, 9, 12, 16, 8, 8])[None, :, None]))[..., None], RO, axis=3)
    wt = 15 * rng.integers(0, 2, (N, 8, 16)); wt[:, 7] = 0
    full = np.array([15] * 8 + [9] + [0] * 7); wt[:, 6] = full[o[:, 6]]; wt[:, 0] = full[o[:, 0]]
    c = np.array([0, 3, L - 1]); lots[:, 6, 0, c] = W - 1; lots[:, 6, 15, c] = W - 1
    v = np.arange(W)
    back = lambda t, to: int(np.argmax(((v + (v >> 5) + 77 * (t + 1)) & (W - 1)) == to))
    lots[:, 7, 0, c] = W - 1; lots[:, 7, 1, c] = back(0, W - 1); lots[:, 7, 2, c] = back(0, back(1, W - 1))
    return pack(price, packs, prev, lots, inc, wt, slack)
def setup_inputs_corners(rng):
    price, packs, prev, lots, inc, wt, slack = base(rng); a = np.arange(H0)
    kinds = [a, np.maximum(a - 1, 0), 0 * a, 0 * a + H0 - 1, (a + 1) % H0, a ^ 1, H0 - L + a % L]
    for q in range(N):
        for g, k in enumerate(rng.permutation(8)):
            if k < 7: prev[q, g] = kinds[int(k)]
            wt[q, g] = (0, 15, 1, 7)[int(rng.integers(0, 4))] if k < 4 else wt[q, g]
            inc[q, g] = 1 if k % 3 == 0 else 7 if k % 3 == 1 else inc[q, g]
    s = [int(g) for g in rng.permutation(8)]
    for g in s[:4]: slack[:, g] = 255
    lots[:, s[0], :RO] = W - 1; wt[:, s[0]] = 0; price[:, s[0], :, W - 1] = 127; inc[:, s[0]] = 7
    lots[:, s[1], 0] = 0; price[:, s[1], :, 0] = 127 * rng.integers(0, 2, (N, 16))
    m = rng.permutation(W); lots[:, s[2], 0] = m[(np.arange(N * L) % (W - 1) + 1).reshape(N, L)]; lots[int(rng.integers(0, N)), s[2], 0, L - 1] = m[0]
    for q in range(N): lots[q, s[3], 0] = rng.permutation(W)[:L]
    packs[:, s[4], :, H0 - L:] = lots[:, s[4]]
    slack[:, s[4]] = 0; slack[:, s[5]] = 0; h = W // 2
    price[:, s[5], :, :h] = rng.integers(0, 3, (N, 16, h)); price[:, s[5], :, h:] = 127; lots[:, s[5]] = rng.integers(h, W, (N, 16, L)); packs[:, s[5]] = rng.integers(0, h, (N, 16, H0))
    nxt = lambda z, u, t: (((z * (2 * u + 1)) >> 5) + z + 77 * (t + 1)) & (W - 1)
    g = s[6]; b = int(rng.integers(0, N)); k = L // 2
    wt[:, g] = 0; inc[:, g] = 7; inc[b, g] = 1 + rng.permutation(16) % 5
    slack[:, g] = 255; slack[:, g, :, RO - 1] = 254 - rng.integers(0, 55, (N, 16)) * (np.arange(N) % 2)[:, None]
    e = rng.integers(0, W, L); own = nxt(e, 0, 0); own[k:] = nxt(own[k:], 0, 1)
    lots[:, g, 0] = own; lots[:, g, 1, :k] = e[:k]; lots[:, g, 2, k:] = e[k:]
    dear = np.zeros(W, bool); dear[own] = True; low = rng.random(W) < 0.5
    v = 200 - (rng.random((N, 16, W)) * np.where(low, 32, 8)).astype(np.int64)
    v[b] = np.where(low, rng.integers(0, 4, (16, W)), v[b])
    price[:, g] = np.where(dear, v, rng.integers(0, 3, W))
    g = s[7]; wt[:, g] = 15; inc[:, g] = 7; slack[:, g] = 255; price[:, g] = 200
    e = rng.integers(0, W, L); lots[:, g, 1] = e; lots[:, g, 0] = nxt(e, (16 * 15 * 200) & 1023, 0)
    return pack(price, packs, prev, lots, inc, wt, slack)
def setup_inputs_ties(rng):
    price, packs, prev, lots, inc, wt, slack = base(rng)
    s0 = rng.integers(0, 21, (N, 8, 16)); b = rng.integers(0, 106, (N, 8, 16)); slack = np.repeat(s0[..., None], RO, axis=3)
    n = rng.choice(np.array([0, 7, 8, 9, 10, 16]), (N, 8, 1, W)); low = rng.random((N, 8, 1, W)) < 0.5
    o = np.argsort(rng.random((N, 8, W, 16)), axis=3).transpose(0, 1, 3, 2)
    price = b[..., None] + np.where(low, 0, s0[..., None] + (o < n))
    return pack(price, packs, prev, lots, inc, wt, slack)
def check_inputs(d):
    bad = []
    for k, lo, hi in (("price", 0, 200), ("packs", 0, W - 1), ("prev", 0, H0 - 1), ("lots", 0, W - 1), ("inc", 1, 7), ("wt", 0, 15), ("slack", 0, 255)):
        v = np.asarray(d[k]).astype(np.float64)
        if not (np.min(v) >= lo and np.max(v) <= hi): bad.append("range of " + k)
        elif np.any(v != np.floor(v)): bad.append("whole numbers in " + k)
    return bad
def pick(p, t):
    return np.take_along_axis(p, t.reshape(N, 8, 1, 16 * L), 3).reshape(N, 8, 16, 16, L)
def reference(price, packs, prev, lots, inc, wt, slack):
    p = price.astype(np.float32).astype(np.int64).reshape(N, 8, 16, W)
    h = np.zeros((N, 8, 16, H0 + RO * L), np.int64); h[..., :H0] = packs.reshape(N, 8, 16, H0)
    v = np.zeros((N, 8, H0 + RO * L), np.int64); v[..., :H0] = prev
    t = lots.astype(np.int64).reshape(N, 8, 16, L)
    up = inc.astype(np.int64).reshape(N, 8, 16, 1); wr = wt.astype(np.int64).reshape(N, 8, 16, 1); sl = slack.astype(np.int64).reshape(N, 8, 16, RO)
    a = np.zeros((N, 8, L), np.int64) + (H0 - L + np.arange(L))
    for rnd in range(RO):
        x = pick(p, t); bind = np.zeros((N, 8, L), np.int64) - 1
        for e in range(Q):
            anc = np.take_along_axis(h, a[:, :, None, :], 3); y = pick(p, anc)
            rows = np.add.reduce((x - y > sl[:, :, :, rnd][:, :, :, None, None]).astype(np.int64), axis=2)
            rev = rows >= 9
            t = np.where(rev, anc, t); x = np.where(rev[:, :, None], y, x)
            bind = np.where(np.any(rev, axis=2), a, bind); last = a
            a = np.take_along_axis(v, a, 2)
        lo = H0 + L * rnd
        h[..., lo:lo + L] = t; v[..., lo:lo + L] = np.where(bind >= 0, bind, last)
        flag = np.zeros((N, 8, W), np.int64); np.put_along_axis(flag, t[:, :, rnd], 1, 2)
        offer = p * flag[:, :, None]; s = np.add.reduce(offer, axis=0)[None] - offer
        if rnd + 1 < RO:
            u = np.add.reduce(wr * np.max(x, axis=3), axis=2) & 1023
            t = (((t * (2 * u + 1)[:, :, None]) >> 5) + t + 77 * (rnd + 1)) & (W - 1)
            a = np.zeros((N, 8, L), np.int64) + (lo + np.arange(L))
        p = np.minimum(p + ((up * s) >> 6), 255)
    return {"yp": p.reshape(N, 128, W).astype(np.float32).astype(BF), "yh": np.ascontiguousarray(h[..., H0:]).reshape(N, 128, RO * L).astype(np.float32), "yv": np.ascontiguousarray(v[..., H0:]).astype(np.float32)}

@@ -1,0 +1,571 @@
+from concourse.bass import DstId, RemoteDMATransfer
+from concourse.mybir import AluOpType, ActivationFunctionType
+
+OFFS, BIG = 131072, 16384
+W, L, H0 = 2048, 256, 768
+NCH, CW = 4, 64
+NB = 2
+BW = W // NB
+BF, F32, I32, U16, F16 = "bfloat16", "float32", "int32", "uint16", "float16"
+CYC = 0.83e-3 * 1.2
+LAT, HOT, XT, XT1 = 0.1, 500.0, 16.0, 14.0
+DH, DM = 0.1, 0.03
+SPLIT = 2
+
+SCRATCH = {
+    "P0": ("sbuf", [128, W], BF), "P1": ("sbuf", [128, W], BF), "P2": ("sbuf", [128, W], BF),
+    "ps0": ("sbuf", [128, W], BF), "ps1": ("sbuf", [128, W], BF),
+    "pk": ("sbuf", [128, H0], I32), "pv": ("sbuf", [128, H0], I32), "lt": ("sbuf", [128, L], I32),
+    "lc": ("sbuf", [128, 16], I32), "ac": ("sbuf", [128, 16], I32),
+    "ic": ("sbuf", [128, 1], I32), "wc": ("sbuf", [128, 1], I32), "sc": ("sbuf", [128, 2], I32),
+    "icf": ("sbuf", [128, 1], F32), "wcf": ("sbuf", [128, 1], F32), "scf": ("sbuf", [128, 2], F32),
+    "ip": ("sbuf", [128, 1], I32), "im": ("sbuf", [128, 128], I32), "iH": ("sbuf", [128, W], BF), "ik": ("sbuf", [128, 1024], BF),
+    "pg": ("sbuf", [128, 1], I32), "pgf": ("sbuf", [128, 1], F32), "pg16": ("sbuf", [128, 1], F32), "ipf": ("sbuf", [128, 1], F32),
+    "pl": ("sbuf", [128, 1], I32), "plf": ("sbuf", [128, 1], F32), "mg": ("sbuf", [128, 128], I32),
+    "Z": ("sbuf", [128, 144], BF), "Zh": ("sbuf", [128, 144], F16), "BR": ("sbuf", [128, 128], F16),
+    "BDw": ("sbuf", [128, 128], BF), "IB": ("sbuf", [128, 128], BF), "IL": ("sbuf", [128, 128], BF),
+    "ID": ("sbuf", [128, 128], BF), "DG": ("sbuf", [128, 128], BF), "E": ("sbuf", [128, W], BF),
+    "scd": ("sbuf", [128, 1024], BF), "LT": ("sbuf", [128, 16], F32),
+    "pvh": ("sbuf", [128, H0], F16), "vt": ("sbuf", [128, H0], F32), "btab": ("sbuf", [128, 6 * L], F32),
+    "Btab": ("sbuf", [128, 512 + 6 * L], F32), "bh": ("sbuf", [128, 6 * L], F16), "lst": ("sbuf", [128, 6 * 16], U16),
+    "A16": ("sbuf", [128, 8 * L], U16), "AC": ("sbuf", [128, 8 * L], F32), "Bf": ("sbuf", [128, 4 * L], F32),
+    "A16c": ("sbuf", [128, 8 * 16], U16), "ACc": ("sbuf", [128, 8 * 16], F32),
+    "T16": ("sbuf", [128, 2 * L], U16), "TT": ("sbuf", [128, 2 * L], I32), "Lr": ("sbuf", [128, 2 * L], I32),
+    "T16c": ("sbuf", [128, 32], U16), "TTc": ("sbuf", [128, 32], I32), "Lc": ("sbuf", [128, 16], I32),
+    "x": ("sbuf", [128, 4096 + 256], BF), "mk": ("sbuf", [128, 4096 + 256], BF), "sm": ("sbuf", [128, 4096], BF),
+    "yhf": ("sbuf", [128, 2 * L], F32), "Q": ("sbuf", [128, L], I32),
+    "w1": ("sbuf", [128, L], I32), "w2": ("sbuf", [128, L], I32), "w3": ("sbuf", [128, L], I32), "w4": ("sbuf", [128, L], I32),
+    "w5": ("sbuf", [128, L], I32),
+    "hi": ("sbuf", [128, 2 * L], I32), "hb": ("sbuf", [128, 2 * L], BF), "hm": ("sbuf", [128, 512], BF),
+    "Y": ("sbuf", [128, 4 * 144], BF), "e1": ("sbuf", [128, 32], F32), "e2": ("sbuf", [128, 32], F32), "e3": ("sbuf", [128, 32], F32),
+    "el": ("sbuf", [128, 32], U16), "ctab": ("sbuf", [128, 4 * L], F32), "par": ("sbuf", [128, L], F32),
+    "hl": ("sbuf", [128, 64], I32), "hlb": ("sbuf", [128, 64], F32),
+    "OH": ("sbuf", [128, 16 * 128], BF), "OL": ("sbuf", [128, 16 * 128], BF), "C": ("sbuf", [128, 256], BF),
+    "O0": ("sbuf", [128, W], BF), "O1": ("sbuf", [128, W], BF), "N16": ("sbuf", [128, W], F16),
+    "LO0": ("sbuf", [128, 3 * W], BF), "LO1": ("sbuf", [128, 3 * W], BF),
+    "HB": ("sbuf", [128, 2 * W], BF),
+}
+for _i in range(8):
+    SCRATCH["pb%d" % _i] = ("psum", [128, 512], F32)
+ND = 48
+SEMAPHORES = ["qv", "qs", "qt", "qg", "snd", "hs"] + ["d%d" % i for i in range(ND)] + \
+    ["%s%d_%d" % (n, t, b) for n in ("arr", "hin") for t in range(2) for b in range(NB)]
+
+A = AluOpType
+AF = ActivationFunctionType
+
+
+def build():
+    ops = []
+    hot = [0.0]
+
+    def add(q, cost, fn, rd, wr, kind="c", tag=""):
+        ops.append({"q": q, "cost": cost, "fn": fn, "rd": rd, "wr": wr, "kind": kind, "tag": tag, "hot": hot[0]})
+
+    def vc(n, cyc=1.0):
+        return max(64, n * cyc) * CYC + 0.01
+
+    def ga(n):
+        return n * 1.55 * CYC + 0.06
+
+    def S(T, r):
+        return T[r[0]][:, r[1]:r[2]] if len(r) == 3 else T[r[0]][:, r[1]:r[2]:r[3]]
+
+    def n_of(r):
+        return len(range(*r[1:]))
+
+    def copy(out, in_, cyc=1.0, tag=""):
+        add("v", vc(n_of(out), cyc), lambda g, T, X: g.vector.tensor_copy(S(T, out), S(T, in_)), [in_], [out], tag=tag)
+
+    def ts(out, in_, s1, op0, s2=None, op1=None, cyc=1.0, tag=""):
+        rd = [in_] + [s for s in (s1, s2) if isinstance(s, tuple)]
+
+        def fn(g, T, X):
+            a = S(T, s1) if isinstance(s1, tuple) else s1
+            b = S(T, s2) if isinstance(s2, tuple) else s2
+            if op1 is None:
+                return g.vector.tensor_scalar(S(T, out), S(T, in_), a, None, op0)
+            return g.vector.tensor_scalar(S(T, out), S(T, in_), a, b, op0, op1)
+        add("v", vc(n_of(out), cyc), fn, rd, [out], tag=tag)
+
+    def tt(out, a, b, op, tag=""):
+        two = 1.0 if (a[0][:2] == "pb" or b[0][:2] == "pb") else 2.0
+        add("v", vc(n_of(out), two), lambda g, T, X: g.vector.tensor_tensor(S(T, out), S(T, a), S(T, b), op), [a, b], [out], tag=tag)
+
+    def act(out, in_, bias=0.0, tag=""):
+        def fn(g, T, X):
+            if bias:
+                return g.scalar.activation(S(T, out), S(T, in_), AF.Copy, bias=bias)
+            return g.scalar.activation(S(T, out), S(T, in_), AF.Copy)
+        add("s", n_of(out) * CYC + 0.06, fn, [in_], [out], tag=tag)
+
+    def gath(q, out, win, off, tag=""):
+        def fn(g, T, X):
+            i = S(T, win).indirect(S(T, off))
+            return g.vector.tensor_copy(S(T, out), i) if q == "v" else g.scalar.activation(S(T, out), i, AF.Copy)
+        add(q, ga(n_of(out)), fn, [win, off], [out], tag=tag)
+
+    def mm(out, pairs, tag="", k=128):
+        def fn(g, T, X):
+            r = None
+            for i, (l, h) in enumerate(pairs):
+                a, b = (S(T, l), S(T, h)) if k == 128 else (T[l[0]][0:k, l[1]:l[2]], T[h[0]][0:k, h[1]:h[2]])
+                r = g.tensor.matmul(S(T, out), a, b, i == 0, i == len(pairs) - 1)
+            return r
+        add("t", sum(max(64, n_of(h)) for l, h in pairs) * CYC * 0.9 + 0.06, fn, [p for lh in pairs for p in lh], [out], tag=tag)
+
+    def dma(out, in_, kb, rd, wr, q="y", tag=""):
+        def fn(g, T, X):
+            return (g.sync if q == "y" else g.scalar).dma_start(out(T), in_(T))
+        add(q, 2.0 + kb / 180.0, fn, rd, wr, kind="d", tag=tag)
+
+    def iota(out, pattern, base, cm, small=False):
+        n = n_of(out)
+
+        def fn(g, T, X):
+            if small:
+                return g.iota(S(T, out), pattern, base, cm, allow_small_or_imprecise_dtypes=True)
+            return g.iota(S(T, out), pattern, base, cm)
+        add("g", 0.15 + 2 * n * CYC, fn, [], [out])
+
+    def mset(out, v):
+        add("v", vc(n_of(out)), lambda g, T, X: g.vector.memset(S(T, out), v), [], [out])
+
+    R = lambda b, n, a=0: (b, a, a + n)
+
+    hot[0] = 2000.0
+    dma(lambda T: T["pv"][0:8, :], lambda T: T.prev[:], 24, [], [R("pv", H0)], q="s")
+    hot[0] = 1990.0
+    dma(lambda T: T["lc"][:], lambda T: T.lots[0::16, :], 8, [], [R("lc", 16)])
+    hot[0] = 1985.0
+    dma(lambda T: T["P0"][:, 0:W], lambda T: T.price[:], 512, [], [R("P0", W)], q="s")
+    hot[0] = 1980.0
+    dma(lambda T: T["sc"][:], lambda T: T.slack[:], 1, [], [R("sc", 2)])
+    dma(lambda T: T["ac"][:], lambda T: T.packs[0::16, H0 - L:H0], 8, [], [R("ac", 16)])
+    dma(lambda T: T["lt"][:], lambda T: T.lots[:], 128, [], [R("lt", L)])
+    hot[0] = 1970.0
+    dma(lambda T: T["pk"][:], lambda T: T.packs[:], 384, [], [R("pk", H0)])
+    hot[0] = 0.0
+    dma(lambda T: T["wc"][:], lambda T: T.wt[:], 1, [], [R("wc", 1)])
+    dma(lambda T: T["ic"][:], lambda T: T.inc[:], 1, [], [R("ic", 1)])
+    iota(R("ip", 1), [[1, 1]], 0, 1)
+    iota(R("im", 128), [[1, 128]], 0, 0)
+    iota(R("btab", L), [[1, L]], H0 - L, 0, True)
+    iota(R("ik", 1024), [[0, 64], [1, 16]], 0, 0, True)
+    hot[0] = -HOT
+    iota(R("iH", W), [[1, 16], [16, 8], [0, 16]], 0, 0, True)
+    iota(R("ctab", L), [[1, L]], H0, 0, True)
+    hot[0] = HOT
+    mset(R("Z", 144), 0.0)
+    ts(R("pg", 1), R("ip", 1), 4, A.logical_shift_right)
+    copy(R("ipf", 1), R("ip", 1))
+    copy(R("pgf", 1), R("pg", 1))
+    ts(R("mg", 128), R("im", 128), 4, A.logical_shift_right)
+    ts(("Z", 15, 128, 16), R("im", 8), R("pgf", 1), A.is_equal, float(BIG), A.mult)
+    ts(R("BR", 128), R("mg", 128), R("ipf", 1), A.is_equal)
+    ts(R("Zh", 144), R("Z", 144), 1.0 / BIG, A.mult)
+    hot[0] = 0.0
+    ts(R("pg16", 1), R("pg", 1), 16.0, A.mult)
+    ts(R("IB", 128), R("im", 128), R("pg16", 1), A.subtract)
+    copy(R("IL", 128), R("im", 128))
+    ts(R("E", W), R("iH", W), R("ipf", 1), A.is_equal, cyc=0.5)
+    ts(R("ID", 128), R("im", 128), R("ipf", 1), A.is_equal)
+    ts(R("icf", 1), R("ic", 1), 1.0 / 64, A.mult)
+    ts(R("DG", 128), R("im", 128), R("ipf", 1), A.is_equal, R("icf", 1), A.mult)
+    copy(R("wcf", 1), R("wc", 1))
+    ts(R("BDw", 128), R("mg", 128), R("pgf", 1), A.is_equal, R("wcf", 1), A.mult)
+    ts(R("scd", 1024), R("ik", 1024), 1.0, A.min, cyc=0.5)
+    ts(R("pl", 1), R("ip", 1), 15, A.bitwise_and)
+    copy(R("plf", 1), R("pl", 1))
+    ts(R("LT", 16), R("im", 16), 16.0, A.mult, R("plf", 1), A.add)
+    ts(R("LT", 16), R("LT", 16), -256.0, A.add)
+    for i in range(4):
+        mset(R("Y", 144, 144 * i), 0.0)
+    con = [float(2048 * (e + 1) + OFFS) for e in range(4)]
+    hot[0] = 4 * HOT
+    copy(R("T16c", 16), R("lc", 16))
+    hot[0] = 3 * HOT
+    copy(R("A16c", 16), R("ac", 16))
+    copy(R("scf", 2), R("sc", 2))
+    ts(R("ps0", W), R("P0", W), ("scf", 0, 1), A.add, 255.0, A.min, cyc=0.5)
+    ts(R("ACc", 16), R("ac", 16), con[0], A.add)
+    ts(R("TTc", 16), R("lc", 16), float(OFFS), A.add)
+    hot[0] = HOT
+    for o, n in ((512, 256), (0, 512)):
+        add("v", vc(n), lambda g, T, X, o=o, n=n: g.vector.tensor_copy(T["pvh"][0:8, o:o + n], T["pv"][0:8, o:o + n]), [R("pv", n, o)], [R("pvh", n, o)])
+    mm(R("pb1", 256), [(R("BR", 128), R("pvh", 256, 512))], k=8)
+    mm(R("pb0", 512), [(R("BR", 128), R("pvh", 512))], k=8)
+    copy(R("bh", L, L), R("pb1", 256))
+    act(R("vt", 256, 512), R("pb1", 256))
+    act(R("vt", 512), R("pb0", 512))
+    hot[0] = 2 * HOT
+    copy(R("T16", L), R("lt", L))
+    copy(R("A16", L), R("pk", L, H0 - L))
+    hot[0] = HOT
+    copy(R("Btab", H0), R("pk", H0))
+    hot[0] = 0.0
+    ts(R("TT", L), R("lt", L), float(OFFS), A.add)
+    act(R("AC", L), R("Btab", L, 512), con[0])
+    hot[0] = -HOT
+    act(R("btab", L, L), R("vt", L, 512))
+
+    def lot_forms(i, src, e):
+        copy(R("A16", L, L * i), src, tag="A16")
+        act(R("AC", L, L * i), src, con[e], tag="AC")
+        claim_forms(i, i // 4)
+
+    def claim_forms(i, t):
+        dma(lambda T: T["A16c"][:, 16 * i:16 * i + 16], lambda T: T["A16"][t::16, L * i:L * i + L], 8, [R("A16", L, L * i)], [R("A16c", 16, 16 * i)])
+        dma(lambda T: T["ACc"][:, 16 * i:16 * i + 16], lambda T: T["AC"][t::16, L * i:L * i + L], 8, [R("AC", L, L * i)], [R("ACc", 16, 16 * i)])
+
+    def chain(e):
+        hot[0] = HOT if e < 4 else 0.0
+        mm(R("pb7", 16), [(R("Zh", 128, 15 - s), ("bh", L * e + s, L * e + L, 16)) for s in range(16)], tag="list")
+        ts(R("lst", 16, 16 * e), R("pb7", 16), 1.0 / 16, A.mult)
+        if e < 5:
+            gath("v", R("bh", L, L * (e + 1)), R("vt", H0), R("lst", 16, 16 * e))
+        gath("s", R("Btab", L, 512 + L * e), R("Btab", H0), R("lst", 16, 16 * e))
+        if e < 4:
+            lot_forms(e, R("Btab", L, 512 + L * e), e)
+        hot[0] = -HOT
+        if e < 5:
+            gath("s", R("btab", L, L * (e + 1)), R("vt", H0), R("lst", 16, 16 * e))
+        hot[0] = 0.0
+
+    for e in range(1, 4):
+        chain(e)
+
+    def trial(t, e, c):
+        i = 4 * t + e
+        if c is None:
+            w, xo, pb, parts = 16, 4096, "pb6", 1
+            a16, acd, t16, tcd, l = R("A16c", 16, 16 * i), R("ACc", 16, 16 * i), R("T16c", 16, 16 * t), R("TTc", 16, 16 * t), R("Lc", 16)
+        else:
+            w, xo, pb, parts = CW, 16 * CW * c, "pb%d" % (3 + c % 3), SPLIT
+            a16, acd = R("A16", w, L * i + w * c), R("AC", w, L * i + w * c)
+            t16, tcd, l = R("T16", w, L * t + w * c), R("TT", w, L * t + w * c), R("Lr", w, L * t + w * c)
+        n, ps = 16 * w, "ps%d" % t
+        tag = "t%d%d%s" % (t, e, c)
+        for s in range(parts):
+            nn, ww = n // parts, w // parts
+            xs, ts_, as_ = R("x", nn, xo + nn * s), R(t16[0], ww, t16[1] + ww * s), R(a16[0], ww, a16[1] + ww * s)
+            gath("s", xs, R("P%d" % t, W), ts_, tag="x" + tag)
+            add("v", ga(nn), lambda g, T, X, xs=xs, as_=as_: g.vector.tensor_tensor(T["mk"][:, xs[1]:xs[2]], T[ps][:, 0:W].indirect(S(T, as_)), S(T, xs), A.is_lt),
+                [R(ps, W), as_, xs], [("mk", xs[1], xs[2])], tag="m" + tag)
+        mm(R(pb, w), [(R("Z", 128, 15 - k), ("mk", xo + k, xo + n, 16)) for k in range(16)], tag="c" + tag)
+        tt(R(pb, w, 128), R(pb, w), acd, A.min)
+        tt(tcd, R(pb, w, 128), tcd, A.max)
+        if c is not None or e < 3:
+            ts(l, tcd, 2047, A.bitwise_and)
+        if e < 3 or (t == 0 and c is not None):
+            copy(t16, l)
+
+    def claims(t):
+        P, O, LO = "P%d" % t, "O%d" % t, "LO%d" % t
+        ts(R("hl", 16, 32 * t), R("TTc", 16, 16 * t), 7, A.logical_shift_right, 15, A.bitwise_and)
+        ts(R("hl", 16, 32 * t + 16), R("TTc", 16, 16 * t), 127, A.bitwise_and)
+        copy(R("hlb", 32, 32 * t), R("hl", 32, 32 * t))
+        for s in range(16):
+            ts(R("OH", 128, 128 * s), R("IB", 128), R("hlb", 1, 32 * t + s), A.is_equal, cyc=0.5)
+            ts(R("OL", 128, 128 * s), R("IL", 128), R("hlb", 1, 32 * t + 16 + s), A.is_equal, cyc=0.5)
+        mm(R("pb7", 128), [(R("OH", 128, 128 * s), R("OL", 128, 128 * s)) for s in range(16)], tag="C%d" % t)
+        ts(R("C", 128, 128 * t), R("pb7", 128), 1.0, A.min)
+        for b in range(4):
+            pb = "pb%d" % (b % 3)
+
+            def fn(g, T, X, b=b, pb=pb):
+                r = None
+                for h in range(4):
+                    r = g.tensor.matmul(T[pb][:, 128 * h:128 * h + 128], T["E"][:, 128 * (4 * b + h):128 * (4 * b + h) + 128],
+                                        T["C"][:, 128 * t:128 * t + 128], True, True)
+                return r
+            add("t", 512 * CYC, fn, [R("E", 512, 512 * b), R("C", 128, 128 * t)], [R(pb, 512)], tag="F")
+            tt(R(O, 512, 512 * b), R(pb, 512), R(P, 512, 512 * b), A.mult, tag="O")
+            if (b + 1) * 512 % BW == 0:
+                k = ((b + 1) * 512 - 1) // BW
+                add("g", 1.0, lambda g, T, X, k=k: X["send"](g, T, t, k), [R(O, BW, BW * k)], [("wire%d" % t, k, k + 1)], kind="r", tag="send")
+                add("x%d%d" % (t, k), (XT, XT1)[t] + 3.0 * k, "arr%d_%d" % (t, k), [("wire%d" % t, k, k + 1)],
+                    [R(LO, BW, q * W + BW * k) for q in range(3)], kind="x", tag="arrive")
+
+    def prices(t):
+        P, N, LO = "P%d" % t, "P%d" % (t + 1), "LO%d" % t
+        for b in range(4):
+            o, pb = 512 * b, "pb%d" % (b % 3)
+            mm(R(pb, 512), [(R("ID", 128), R(P, 512, o))] + [(R("DG", 128), R(LO, 512, q * W + o)) for q in range(3)], tag="W")
+            ts(R("N16", 512, o), R(pb, 512), 1025.0 - 63.0 / 128, A.add, 1280.0, A.min)
+            ts(R(N, 512, o), R("N16", 512, o), -1025.0, A.add, cyc=0.5)
+            if t == 0:
+                ts(R("ps1", 512, o), R(N, 512, o), ("scf", 1, 2), A.add, 255.0, A.min, cyc=0.5)
+            else:
+                dma(lambda T, o=o: T.yp[:, o:o + 512], lambda T, o=o: T["P2"][:, o:o + 512], 128, [R("P2", 512, o)], [], q="ys"[b % 2])
+
+    def parents(t):
+        for h in range(2):
+            o, k = L * t + 128 * h, 2 * t + h
+            ts(R("hi", 128, o), R("TT", 128, o), 11, A.logical_shift_right, 7, A.bitwise_and)
+            copy(R("hb", 128, o), R("hi", 128, o))
+            mm(R("pb7", 128), [(R("hb", 128, o), R("ID", 128))], tag="hT")
+            add("v", vc(128), lambda g, T, X, k=k: g.vector.tensor_tensor_scan(T["hm"][:, 128 * k:128 * k + 128], T["scd"][:, 0:128], T["pb7"][:, 0:128], 0.0, A.mult, A.max),
+                [R("scd", 128), R("pb7", 128)], [R("hm", 128, 128 * k)])
+            ts(("Y", 144 * k + 15, 144 * k + 128, 16), ("hm", 128 * k + 15, 128 * k + 128, 16), 256.0, A.mult)
+
+        def fn(g, T, X):
+            r = None
+            for h in range(2):
+                y = 144 * (2 * t + h)
+                for s in range(16):
+                    r = g.tensor.matmul(T["pb7"][:, 8 * h:8 * h + 8], T["Y"][:, y + 15 - s:y + 143 - s], T["ID"][:, s:128:16], s == 0, s == 15)
+            return r
+        add("t", 2048 * CYC * 0.9, fn, [R("Y", 288, 288 * t), R("ID", 128)], [R("pb7", 16)], tag="elist")
+        ts(R("e1", 16, 16 * t), R("pb7", 16), 0.0, A.is_equal, 1024.0, A.mult)
+        tt(R("e2", 16, 16 * t), R("pb7", 16), R("e1", 16, 16 * t), A.add)
+        tt(R("e3", 16, 16 * t), R("e2", 16, 16 * t), R("LT", 16), A.add)
+        copy(R("el", 16, 16 * t), R("e3", 16, 16 * t))
+
+    hot[0] = HOT
+    for e in range(4):
+        trial(0, e, None)
+    claims(0)
+    chain(4)
+    chain(5)
+    for e in range(4):
+        for c in range(NCH):
+            trial(0, e, c)
+    prices(0)
+    for c in range(NCH):
+        r = lambda b, k=0: R(b, CW, k + CW * c)
+        n = 16 * CW
+        gath("s", R("x", n, n * c), R("P0", W), r("T16"), tag="x04%d" % c)
+        add("v", vc(n, 0.5), lambda g, T, X, c=c, n=n: g.vector.tensor_tensor_scan(T["sm"][:, n * c:n * c + n], T["scd"][:, 0:n], T["x"][:, n * c:n * c + n], 0.0, A.mult, A.max),
+            [R("scd", n), R("x", n, n * c)], [R("sm", n, n * c)], tag="scan")
+        mm(R("pb7", CW), [(R("BDw", 128), ("sm", n * c + 15, n * c + n, 16))], tag="u")
+        ts(r("Q"), r("Lr"), 32.0, A.mult, 2464.0, A.add)
+        ts(r("w1"), R("pb7", CW), 2.0, A.mult, 1.0, A.add)
+        ts(r("w2"), r("w1"), 2047, A.bitwise_and)
+        tt(r("w3"), r("w2"), r("Lr"), A.mult)
+        tt(r("w4"), r("w3"), r("Q"), A.add)
+        ts(r("w5"), r("w4"), 5, A.logical_shift_right, 2047, A.bitwise_and)
+        copy(r("T16", L), r("w5"))
+        ts(r("TT", L), r("w5"), float(OFFS), A.add)
+        copy(r("A16", 4 * L), r("Lr"))
+        copy(r("yhf"), r("Lr"))
+        act(r("AC", 4 * L), r("yhf"), con[0])
+    dma(lambda T: T.yh[:, 0:L], lambda T: T["yhf"][:, 0:L], 128, [R("yhf", L)], [])
+    hot[0] = HOT / 2
+    dma(lambda T: T["T16c"][:, 16:32], lambda T: T["T16"][1::16, L:2 * L], 8, [R("T16", L, L)], [R("T16c", 16, 16)])
+    dma(lambda T: T["TTc"][:, 16:32], lambda T: T["TT"][1::16, L:2 * L], 8, [R("TT", L, L)], [R("TTc", 16, 16)])
+    claim_forms(4, 1)
+    parents(0)
+    for e in (1, 2, 3):
+        gath("s", R("Bf", L, L * e), R("Btab", 4 * L, 512 + L * (e - 1)), R("el", 16))
+        lot_forms(4 + e, R("Bf", L, L * e), e)
+    hot[0] = -HOT
+    for j in range(3):
+        gath("s", R("ctab", L, L * (j + 1)), R("btab", 4 * L, L * j), R("el", 16))
+    dma(lambda T: T.yv[:, 0:L], lambda T: T["ctab"][0::16, L:2 * L], 8, [R("ctab", L, L)], [])
+    hot[0] = HOT
+    for e in range(4):
+        trial(1, e, None)
+    claims(1)
+    hot[0] = 0.0
+    for e in range(4):
+        for c in range(NCH):
+            trial(1, e, c)
+    prices(1)
+    for c in range(NCH):
+        copy(R("yhf", CW, L + CW * c), R("Lr", CW, L + CW * c))
+        if c % 2:
+            o = L + 128 * (c // 2)
+            dma(lambda T, o=o: T.yh[:, o:o + 128], lambda T, o=o: T["yhf"][:, o:o + 128], 64, [R("yhf", 128, o)], [])
+    parents(1)
+    gath("s", R("par", L), R("ctab", 4 * L), R("el", 16, 16))
+    dma(lambda T: T.yv[:, L:2 * L], lambda T: T["par"][0::16, :], 8, [R("par", L)], [])
+    return ops
+
+
+def depend(ops):
+    acc, deps = {}, []
+    for i, o in enumerate(ops):
+        d = set()
+        for wr, rs in ((False, o["rd"]), (True, o["wr"])):
+            for r in rs:
+                for (j, a, b, w) in acc.get(r[0], []):
+                    bank = r[0][:2] == "pb" and ops[j]["q"] != o["q"]
+                    if j != i and (bank or ((w or wr) and a < r[2] and r[1] < b)):
+                        d.add(j)
+        for wr, rs in ((False, o["rd"]), (True, o["wr"])):
+            for r in rs:
+                lst = acc.setdefault(r[0], [])
+                if wr and r[0][:2] != "pb" and len(r) == 3:
+                    lst[:] = [e for e in lst if not (r[1] <= e[1] and e[2] <= r[2] and e[0] in d)]
+                lst.append((i, r[1], r[2], wr))
+        deps.append(sorted(d))
+    return deps
+
+
+def schedule(ops, deps):
+    n = len(ops)
+    succ = [[] for _ in range(n)]
+    for i, d in enumerate(deps):
+        for j in d:
+            succ[j].append(i)
+    lev = [0.0] * n
+    for i in range(n - 1, -1, -1):
+        lev[i] = ops[i]["cost"] + max([lev[k] + LAT for k in succ[i]] or [0.0])
+    wgt = [lev[i] + ops[i]["hot"] for i in range(n)]
+    left = [len(d) for d in deps]
+    ready = [0.0] * n
+    cand, free, order = {}, {}, []
+    for i in range(n):
+        if not left[i]:
+            cand.setdefault(ops[i]["q"], []).append(i)
+    while True:
+        best = None
+        for q, l in cand.items():
+            if l:
+                t = max(free.get(q, 0.0), min(ready[i] for i in l))
+                if best is None or t < best[0]:
+                    best = (t, q)
+        if best is None:
+            break
+        t, q = best
+        i = max((i for i in cand[q] if ready[i] <= t + (DH if ops[i]["hot"] > 0 else DM) + 1e-9), key=lambda i: (wgt[i], -i))
+        t = max(t, ready[i])
+        cand[q].remove(i)
+        o = ops[i]
+        fin = t + o["cost"]
+        if o["kind"] == "d":
+            free["dma"] = max(free.get("dma", 0.0), t) + o["cost"] - 2.0
+            fin = free["dma"] + 2.0
+        free[q] = t + (0.1 if o["kind"] == "d" else o["cost"])
+        order.append(i)
+        for k in succ[i]:
+            left[k] -= 1
+            ready[k] = max(ready[k], fin + LAT)
+            if not left[k]:
+                cand.setdefault(ops[k]["q"], []).append(k)
+    assert len(order) == n
+    return order
+
+
+PLAN = {}
+
+
+def plan():
+    if "ops" not in PLAN:
+        PLAN["ops"] = build()
+        PLAN["deps"] = depend(PLAN["ops"])
+        PLAN["order"] = schedule(PLAN["ops"], PLAN["deps"])
+    return PLAN["ops"], PLAN["deps"], PLAN["order"]
+
+
+def routes(cores, topo):
+    out = []
+    for c in cores:
+        peers = [d for d in cores if d != c and topo.same_plane(c, d)]
+        far = [d for d in cores if d != c and not topo.same_plane(c, d)]
+        mine = sorted(peers + [c]).index(c)
+        hop = {}
+        for k, d in enumerate(far):
+            own = (mine + k) % 2 == 0
+            hop[d] = [h for h in topo.cores_of(c) if h not in cores and topo.may_write(h, d) and (topo.die(h) == topo.die(c)) == own][0]
+        out.append((peers, hop))
+    return out
+
+
+def slot(cores, src, dst):
+    return [c for c in cores if c != dst].index(src)
+
+
+def bits(es):
+    return sum(1 << e for e in es)
+
+
+def onchip(c, peers, topo, h):
+    off = topo.engines(c, peers[0])
+    return [e for e in topo.engines(c, h) if e not in off]
+
+
+def hand_on(g, core, T, topo):
+    cores = list(T.cores)
+    for c, (peers, hop) in zip(cores, routes(cores, topo)):
+        for d, h in hop.items():
+            if h != core:
+                continue
+            es, into = topo.engines(core, d), onchip(c, peers, topo, h)
+            rid, pid = topo.addr(d, core)
+            k = slot(cores, c, d)
+            for t in range(2):
+                for b in range(NB):
+                    g.wait_ge(T.sem["hin%d_%d" % (t, b)], len(into))
+                    o = k * W + BW * b
+                    g.remote_dma(T["LO%d" % t][:, o:o + BW], T["HB"][:, t * W + BW * b:t * W + BW * b + BW],
+                                 T.sem["arr%d_%d" % (t, b)], T.sem["hs"], pid, rid, bits(es))
+            g.wait_ge(T.sem["hs"], 2 * NB * len(es))
+
+
+def rank_program(g, core, T, topo):
+    if T.rank_of(core) is None:
+        hand_on(g, core, T, topo)
+        return
+    cores = list(T.cores)
+    rt = routes(cores, topo)
+    peers, hop = rt[T.rank_of(core)]
+    ops, deps, order = plan()
+    eng = {"v": g.vector, "s": g.scalar, "t": g.tensor, "y": g.sync, "g": g}
+    sent = [0]
+
+    def send(g_, T_, t, b):
+        p, hs = peers[0], list(hop.values())
+        src = T["O%d" % t][:, BW * b:BW * b + BW]
+        dst = lambda h: DstId(rid=topo.addr(h, core)[0], pnc=topo.addr(h, core)[1])
+        k = slot(cores, core, p) * W + BW * b
+        e0, e1 = topo.engines(core, p), onchip(core, peers, topo, hs[0])
+        g.remote_dma_fused([
+            RemoteDMATransfer(dst_ids=[dst(p)], dma_engine_mask=bits(e0), remote_sem=T.sem["arr%d_%d" % (t, b)],
+                              srcs=[src], dsts=[T["LO%d" % t][:, k:k + BW]]),
+            RemoteDMATransfer(dst_ids=[dst(h) for h in hs], dma_engine_mask=bits(e1), remote_sem=T.sem["hin%d_%d" % (t, b)],
+                              srcs=[src], dsts=[T["HB"][:, t * W + BW * b:t * W + BW * b + BW] for h in hs])],
+            local_sem=T.sem["snd"])
+        sent[0] += len(e0) + len(e1)
+
+    arrive = len(topo.engines(peers[0], core)) + sum(len(topo.engines(h[core], core)) for _, h in rt if core in h)
+    X = {"send": send}
+    cnt = {"v": 0, "s": 0, "t": 0, "g": 0}
+    clock = {q: {} for q in eng}
+    done = {}
+    pos = {i: k for k, i in enumerate(order)}
+    nd = 0
+    for i in order:
+        o = ops[i]
+        if o["kind"] == "x":
+            done[i] = (o["fn"], arrive, {o["fn"]: arrive})
+            continue
+        q = o["q"]
+        ck = clock[q]
+        for j in sorted(deps[i], key=lambda j: -pos[j]):
+            if j in done:
+                s, n, c2 = done[j]
+                if ck.get(s, 0) < n:
+                    eng[q].wait_ge(T.sem[s], n)
+                    for k, v in c2.items():
+                        ck[k] = max(ck.get(k, 0), v)
+        ins = o["fn"](g, T, X)
+        if o["kind"] == "c":
+            cnt[q] += 1
+            s, n = "q" + q, cnt[q]
+            ins.then_inc(T.sem[s], 1)
+        elif o["kind"] == "d":
+            s, n = "d%d" % nd, 16
+            nd += 1
+            ins.then_inc(T.sem[s], 16)
+        else:
+            continue
+        c2 = dict(ck)
+        c2[s] = n
+        done[i] = (s, n, c2)
+    for q, n in cnt.items():
+        g.wait_ge(T.sem["q" + q], n)
+    for k in range(nd):
+        g.wait_ge(T.sem["d%d" % k], 16)
+    g.wait_ge(T.sem["snd"], sent[0])

@@ -8,8 +8,10 @@ NB = 2
 BW = W // NB
 BF, F32, I32, U16, F16 = "bfloat16", "float32", "int32", "uint16", "float16"
 CYC = 0.83e-3 * 1.2
-LAT, HOT, XT, XT1 = 0.1, 500.0, 16.0, 14.0
-DH, DM = 0.1, 0.03
+LAT, HOT, XT, XT1, FP = 0.1, 500.0, 14.0, 14.0, 0.6
+DH, DM = 0.1, 0.05
+SMH, JIT, MIX = 2.0, 0.3, 933
+CO = ((0, 0, 0, 0), (0, -1.6, 0, 0))
 SPLIT = 2
 
 SCRATCH = {
@@ -18,8 +20,8 @@ SCRATCH = {
     "pk": ("sbuf", [128, H0], I32), "pv": ("sbuf", [128, H0], I32), "lt": ("sbuf", [128, L], I32),
     "lc": ("sbuf", [128, 16], I32), "ac": ("sbuf", [128, 16], I32),
     "ic": ("sbuf", [128, 1], I32), "wc": ("sbuf", [128, 1], I32), "sc": ("sbuf", [128, 2], I32),
-    "icf": ("sbuf", [128, 1], F32), "wcf": ("sbuf", [128, 1], F32), "scf": ("sbuf", [128, 2], F32),
-    "ip": ("sbuf", [128, 1], I32), "im": ("sbuf", [128, 128], I32), "iH": ("sbuf", [128, W], BF), "ik": ("sbuf", [128, 1024], BF),
+    "icf": ("sbuf", [128, 1], F32), "wcf": ("sbuf", [128, 1], F32), "scf": ("sbuf", [128, 2], F32), "mo": ("sbuf", [128, 1], F32),
+    "ip": ("sbuf", [128, 1], I32), "im": ("sbuf", [128, 128], I32), "on": ("sbuf", [128, W], BF),
     "pg": ("sbuf", [128, 1], I32), "pgf": ("sbuf", [128, 1], F32), "pg16": ("sbuf", [128, 1], F32), "ipf": ("sbuf", [128, 1], F32),
     "pl": ("sbuf", [128, 1], I32), "plf": ("sbuf", [128, 1], F32), "mg": ("sbuf", [128, 128], I32),
     "Z": ("sbuf", [128, 144], BF), "Zh": ("sbuf", [128, 144], F16), "BR": ("sbuf", [128, 128], F16),
@@ -49,7 +51,7 @@ for _i in range(8):
     SCRATCH["pb%d" % _i] = ("psum", [128, 512], F32)
 ND = 48
 SEMAPHORES = ["qv", "qs", "qt", "qg", "snd", "hs"] + ["d%d" % i for i in range(ND)] + \
-    ["%s%d_%d" % (n, t, b) for n in ("arr", "hin") for t in range(2) for b in range(NB)]
+    ["%s%d_%d" % (n, t, b) for n in ("arr", "far", "hin") for t in range(2) for b in range(NB)]
 
 A = AluOpType
 AF = ActivationFunctionType
@@ -99,20 +101,26 @@ def build():
             return g.scalar.activation(S(T, out), S(T, in_), AF.Copy)
         add("s", n_of(out) * CYC + 0.06, fn, [in_], [out], tag=tag)
 
-    def gath(q, out, win, off, tag=""):
+    def relu(out, in_, bias, scale, tag=""):
+        add("s", n_of(out) * CYC + 0.06, lambda g, T, X: g.scalar.activation(S(T, out), S(T, in_), AF.Relu, bias=S(T, bias), scale=scale),
+            [in_, bias], [out], tag=tag)
+
+    def gath(out, win, off, tag="", comp=False):
         def fn(g, T, X):
             i = S(T, win).indirect(S(T, off))
-            return g.vector.tensor_copy(S(T, out), i) if q == "v" else g.scalar.activation(S(T, out), i, AF.Copy)
-        add(q, ga(n_of(out)), fn, [win, off], [out], tag=tag)
+            if comp:
+                return g.scalar.activation(S(T, out), i, AF.Copy, bias=255.0, scale=-1.0)
+            return g.scalar.activation(S(T, out), i, AF.Copy)
+        add("s", ga(n_of(out)), fn, [win, off], [out], tag=tag)
 
-    def mm(out, pairs, tag="", k=128):
+    def mm(out, pairs, tag="", k=128, first=True, last=True):
         def fn(g, T, X):
             r = None
             for i, (l, h) in enumerate(pairs):
                 a, b = (S(T, l), S(T, h)) if k == 128 else (T[l[0]][0:k, l[1]:l[2]], T[h[0]][0:k, h[1]:h[2]])
-                r = g.tensor.matmul(S(T, out), a, b, i == 0, i == len(pairs) - 1)
+                r = g.tensor.matmul(S(T, out), a, b, first and i == 0, last and i == len(pairs) - 1)
             return r
-        add("t", sum(max(64, n_of(h)) for l, h in pairs) * CYC * 0.9 + 0.06, fn, [p for lh in pairs for p in lh], [out], tag=tag)
+        add("t", sum(max(64, n_of(h)) for l, h in pairs) * CYC + 0.06, fn, [p for lh in pairs for p in lh], [out], tag=tag)
 
     def dma(out, in_, kb, rd, wr, q="y", tag=""):
         def fn(g, T, X):
@@ -128,8 +136,11 @@ def build():
             return g.iota(S(T, out), pattern, base, cm)
         add("g", 0.15 + 2 * n * CYC, fn, [], [out])
 
+    def select(out, in_, pattern, cmp, cm):
+        add("g", 0.17 + 2 * n_of(out) * CYC, lambda g, T, X: g.affine_select(S(T, out), S(T, in_), pattern, cmp, 0.0, 0, cm), [in_], [out])
+
     def mset(out, v):
-        add("v", vc(n_of(out)), lambda g, T, X: g.vector.memset(S(T, out), v), [], [out])
+        add("v", vc(n_of(out), 0.5), lambda g, T, X: g.vector.memset(S(T, out), v), [], [out])
 
     R = lambda b, n, a=0: (b, a, a + n)
 
@@ -151,9 +162,12 @@ def build():
     iota(R("ip", 1), [[1, 1]], 0, 1)
     iota(R("im", 128), [[1, 128]], 0, 0)
     iota(R("btab", L), [[1, L]], H0 - L, 0, True)
-    iota(R("ik", 1024), [[0, 64], [1, 16]], 0, 0, True)
+    iota(R("IL", 128), [[1, 128]], 0, 0, True)
+    iota(R("on", W), [[0, W]], 1, 0, True)
+    select(R("ID", 128), R("on", 128), [[-1, 128]], A.is_equal, 1)
+    select(R("scd", 1024), R("on", 1024), [[0, 64], [1, 16]], A.not_equal, 0)
+    select(R("E", W), R("on", W), [[-1, 16], [-16, 8], [0, 16]], A.is_equal, 1)
     hot[0] = -HOT
-    iota(R("iH", W), [[1, 16], [16, 8], [0, 16]], 0, 0, True)
     iota(R("ctab", L), [[1, L]], H0, 0, True)
     hot[0] = HOT
     mset(R("Z", 144), 0.0)
@@ -165,29 +179,25 @@ def build():
     ts(R("BR", 128), R("mg", 128), R("ipf", 1), A.is_equal)
     ts(R("Zh", 144), R("Z", 144), 1.0 / BIG, A.mult)
     hot[0] = 0.0
+    mset(R("mo", 1), -256.0)
     ts(R("pg16", 1), R("pg", 1), 16.0, A.mult)
     ts(R("IB", 128), R("im", 128), R("pg16", 1), A.subtract)
-    copy(R("IL", 128), R("im", 128))
-    ts(R("E", W), R("iH", W), R("ipf", 1), A.is_equal, cyc=0.5)
-    ts(R("ID", 128), R("im", 128), R("ipf", 1), A.is_equal)
     ts(R("icf", 1), R("ic", 1), 1.0 / 64, A.mult)
     ts(R("DG", 128), R("im", 128), R("ipf", 1), A.is_equal, R("icf", 1), A.mult)
     copy(R("wcf", 1), R("wc", 1))
     ts(R("BDw", 128), R("mg", 128), R("pgf", 1), A.is_equal, R("wcf", 1), A.mult)
-    ts(R("scd", 1024), R("ik", 1024), 1.0, A.min, cyc=0.5)
     ts(R("pl", 1), R("ip", 1), 15, A.bitwise_and)
     copy(R("plf", 1), R("pl", 1))
     ts(R("LT", 16), R("im", 16), 16.0, A.mult, R("plf", 1), A.add)
     ts(R("LT", 16), R("LT", 16), -256.0, A.add)
-    for i in range(4):
-        mset(R("Y", 144, 144 * i), 0.0)
+    mset(R("Y", 576), 0.0)
     con = [float(2048 * (e + 1) + OFFS) for e in range(4)]
     hot[0] = 4 * HOT
     copy(R("T16c", 16), R("lc", 16))
     hot[0] = 3 * HOT
     copy(R("A16c", 16), R("ac", 16))
-    copy(R("scf", 2), R("sc", 2))
-    ts(R("ps0", W), R("P0", W), ("scf", 0, 1), A.add, 255.0, A.min, cyc=0.5)
+    ts(R("scf", 2), R("sc", 2), -1.0, A.mult, 255.0, A.add)
+    relu(R("ps0", W), R("P0", W), R("scf", 1), -1.0, tag="ps0")
     ts(R("ACc", 16), R("ac", 16), con[0], A.add)
     ts(R("TTc", 16), R("lc", 16), float(OFFS), A.add)
     hot[0] = HOT
@@ -215,7 +225,8 @@ def build():
         claim_forms(i, i // 4)
 
     def claim_forms(i, t):
-        dma(lambda T: T["A16c"][:, 16 * i:16 * i + 16], lambda T: T["A16"][t::16, L * i:L * i + L], 8, [R("A16", L, L * i)], [R("A16c", 16, 16 * i)])
+        src, a = ("T16", 0) if i == 4 else ("A16", L * i)
+        dma(lambda T: T["A16c"][:, 16 * i:16 * i + 16], lambda T: T[src][t::16, a:a + L], 8, [R(src, L, a)], [R("A16c", 16, 16 * i)])
         dma(lambda T: T["ACc"][:, 16 * i:16 * i + 16], lambda T: T["AC"][t::16, L * i:L * i + L], 8, [R("AC", L, L * i)], [R("ACc", 16, 16 * i)])
 
     def chain(e):
@@ -223,13 +234,11 @@ def build():
         mm(R("pb7", 16), [(R("Zh", 128, 15 - s), ("bh", L * e + s, L * e + L, 16)) for s in range(16)], tag="list")
         ts(R("lst", 16, 16 * e), R("pb7", 16), 1.0 / 16, A.mult)
         if e < 5:
-            gath("v", R("bh", L, L * (e + 1)), R("vt", H0), R("lst", 16, 16 * e))
-        gath("s", R("Btab", L, 512 + L * e), R("Btab", H0), R("lst", 16, 16 * e))
+            gath(R("btab", L, L * (e + 1)), R("vt", H0), R("lst", 16, 16 * e))
+            copy(R("bh", L, L * (e + 1)), R("btab", L, L * (e + 1)))
+        gath(R("Btab", L, 512 + L * e), R("Btab", H0), R("lst", 16, 16 * e))
         if e < 4:
             lot_forms(e, R("Btab", L, 512 + L * e), e)
-        hot[0] = -HOT
-        if e < 5:
-            gath("s", R("btab", L, L * (e + 1)), R("vt", H0), R("lst", 16, 16 * e))
         hot[0] = 0.0
 
     for e in range(1, 4):
@@ -241,24 +250,27 @@ def build():
             w, xo, pb, parts = 16, 4096, "pb6", 1
             a16, acd, t16, tcd, l = R("A16c", 16, 16 * i), R("ACc", 16, 16 * i), R("T16c", 16, 16 * t), R("TTc", 16, 16 * t), R("Lc", 16)
         else:
-            w, xo, pb, parts = CW, 16 * CW * c, "pb%d" % (3 + c % 3), SPLIT
-            a16, acd = R("A16", w, L * i + w * c), R("AC", w, L * i + w * c)
+            w, xo, pb, parts = CW, 16 * CW * c, "pb%d" % (2 + c % 4), SPLIT
+            a16, acd = R("A16", w, L * i + w * c) if i != 4 else R("T16", w, w * c), R("AC", w, L * i + w * c)
             t16, tcd, l = R("T16", w, L * t + w * c), R("TT", w, L * t + w * c), R("Lr", w, L * t + w * c)
         n, ps = 16 * w, "ps%d" % t
         tag = "t%d%d%s" % (t, e, c)
         for s in range(parts):
             nn, ww = n // parts, w // parts
             xs, ts_, as_ = R("x", nn, xo + nn * s), R(t16[0], ww, t16[1] + ww * s), R(a16[0], ww, a16[1] + ww * s)
-            gath("s", xs, R("P%d" % t, W), ts_, tag="x" + tag)
-            add("v", ga(nn), lambda g, T, X, xs=xs, as_=as_: g.vector.tensor_tensor(T["mk"][:, xs[1]:xs[2]], T[ps][:, 0:W].indirect(S(T, as_)), S(T, xs), A.is_lt),
+            gath(xs, R("P%d" % t, W), ts_, tag="x" + tag, comp=True)
+            add("v", ga(nn), lambda g, T, X, xs=xs, as_=as_: g.vector.tensor_tensor(T["mk"][:, xs[1]:xs[2]], T[ps][:, 0:W].indirect(S(T, as_)), S(T, xs), A.is_gt),
                 [R(ps, W), as_, xs], [("mk", xs[1], xs[2])], tag="m" + tag)
         mm(R(pb, w), [(R("Z", 128, 15 - k), ("mk", xo + k, xo + n, 16)) for k in range(16)], tag="c" + tag)
+        h0 = hot[0]
+        hot[0] += SMH if c is not None else 0.0
         tt(R(pb, w, 128), R(pb, w), acd, A.min)
         tt(tcd, R(pb, w, 128), tcd, A.max)
         if c is not None or e < 3:
             ts(l, tcd, 2047, A.bitwise_and)
         if e < 3 or (t == 0 and c is not None):
             copy(t16, l)
+        hot[0] = h0
 
     def claims(t):
         P, O, LO = "P%d" % t, "O%d" % t, "LO%d" % t
@@ -269,33 +281,42 @@ def build():
             ts(R("OH", 128, 128 * s), R("IB", 128), R("hlb", 1, 32 * t + s), A.is_equal, cyc=0.5)
             ts(R("OL", 128, 128 * s), R("IL", 128), R("hlb", 1, 32 * t + 16 + s), A.is_equal, cyc=0.5)
         mm(R("pb7", 128), [(R("OH", 128, 128 * s), R("OL", 128, 128 * s)) for s in range(16)], tag="C%d" % t)
-        ts(R("C", 128, 128 * t), R("pb7", 128), 1.0, A.min)
+        if t == 0:
+            ts(R("C", 128), R("pb7", 128), 1.0, A.min, 256.0, A.mult)
+        else:
+            ts(R("C", 128, 128), R("pb7", 128), 1.0, A.min)
         for b in range(4):
-            pb = "pb%d" % (b % 3)
+            pb, o = "pb%d" % (b % 2), 512 * b
 
-            def fn(g, T, X, b=b, pb=pb):
+            def fn(g, T, X, o=o, pb=pb):
                 r = None
-                for h in range(4):
-                    r = g.tensor.matmul(T[pb][:, 128 * h:128 * h + 128], T["E"][:, 128 * (4 * b + h):128 * (4 * b + h) + 128],
-                                        T["C"][:, 128 * t:128 * t + 128], True, True)
+                for h in range(0, 512, 128):
+                    if t == 0:
+                        g.tensor.matmul(T[pb][:, h:h + 128], T["ID"][:], T[P][:, o + h:o + h + 128], True, False)
+                    r = g.tensor.matmul(T[pb][:, h:h + 128], T["E"][:, o + h:o + h + 128], T["C"][:, 128 * t:128 * t + 128], t == 1, True)
                 return r
-            add("t", 512 * CYC, fn, [R("E", 512, 512 * b), R("C", 128, 128 * t)], [R(pb, 512)], tag="F")
-            tt(R(O, 512, 512 * b), R(pb, 512), R(P, 512, 512 * b), A.mult, tag="O")
+            add("t", 512 * CYC * (2 - t), fn, [R("ID", 128), R(P, 512, o), R("E", 512, o), R("C", 128, 128 * t)], [R(pb, 512)], tag="F")
+            if t == 0:
+                relu(R(O, 512, o), R(pb, 512), R("mo", 1), 1.0, tag="O")
+            else:
+                tt(R(O, 512, o), R(pb, 512), R(P, 512, o), A.mult, tag="O")
             if (b + 1) * 512 % BW == 0:
                 k = ((b + 1) * 512 - 1) // BW
                 add("g", 1.0, lambda g, T, X, k=k: X["send"](g, T, t, k), [R(O, BW, BW * k)], [("wire%d" % t, k, k + 1)], kind="r", tag="send")
-                add("x%d%d" % (t, k), (XT, XT1)[t] + 3.0 * k, "arr%d_%d" % (t, k), [("wire%d" % t, k, k + 1)],
-                    [R(LO, BW, q * W + BW * k) for q in range(3)], kind="x", tag="arrive")
+                for far in (0, 1):
+                    add("x%d%d%d" % (far, t, k), ((XT, XT1)[t] + 3.0 * k) * (FP, 1.0)[far], "%s%d_%d" % (("arr", "far")[far], t, k), [("wire%d" % t, k, k + 1)],
+                        [R(LO, BW, q * W + BW * k) for q in ((0,), (1, 2))[far]], kind="x", tag="arrive")
 
     def prices(t):
         P, N, LO = "P%d" % t, "P%d" % (t + 1), "LO%d" % t
         for b in range(4):
-            o, pb = 512 * b, "pb%d" % (b % 3)
-            mm(R(pb, 512), [(R("ID", 128), R(P, 512, o))] + [(R("DG", 128), R(LO, 512, q * W + o)) for q in range(3)], tag="W")
+            o, pb = 512 * b, "pb%d" % (b % 2)
+            mm(R(pb, 512), [(R("ID", 128), R(P, 512, o)), (R("DG", 128), R(LO, 512, o))], tag="W1", last=False)
+            mm(R(pb, 512), [(R("DG", 128), R(LO, 512, q * W + o)) for q in (1, 2)], tag="W2", first=False)
             ts(R("N16", 512, o), R(pb, 512), 1025.0 - 63.0 / 128, A.add, 1280.0, A.min)
             ts(R(N, 512, o), R("N16", 512, o), -1025.0, A.add, cyc=0.5)
             if t == 0:
-                ts(R("ps1", 512, o), R(N, 512, o), ("scf", 1, 2), A.add, 255.0, A.min, cyc=0.5)
+                relu(R("ps1", 512, o), R(N, 512, o), R("scf", 1, 1), -1.0, tag="ps1")
             else:
                 dma(lambda T, o=o: T.yp[:, o:o + 512], lambda T, o=o: T["P2"][:, o:o + 512], 128, [R("P2", 512, o)], [], q="ys"[b % 2])
 
@@ -308,19 +329,12 @@ def build():
             add("v", vc(128), lambda g, T, X, k=k: g.vector.tensor_tensor_scan(T["hm"][:, 128 * k:128 * k + 128], T["scd"][:, 0:128], T["pb7"][:, 0:128], 0.0, A.mult, A.max),
                 [R("scd", 128), R("pb7", 128)], [R("hm", 128, 128 * k)])
             ts(("Y", 144 * k + 15, 144 * k + 128, 16), ("hm", 128 * k + 15, 128 * k + 128, 16), 256.0, A.mult)
-
-        def fn(g, T, X):
-            r = None
-            for h in range(2):
-                y = 144 * (2 * t + h)
-                for s in range(16):
-                    r = g.tensor.matmul(T["pb7"][:, 8 * h:8 * h + 8], T["Y"][:, y + 15 - s:y + 143 - s], T["ID"][:, s:128:16], s == 0, s == 15)
-            return r
-        add("t", 2048 * CYC * 0.9, fn, [R("Y", 288, 288 * t), R("ID", 128)], [R("pb7", 16)], tag="elist")
-        ts(R("e1", 16, 16 * t), R("pb7", 16), 0.0, A.is_equal, 1024.0, A.mult)
-        tt(R("e2", 16, 16 * t), R("pb7", 16), R("e1", 16, 16 * t), A.add)
-        tt(R("e3", 16, 16 * t), R("e2", 16, 16 * t), R("LT", 16), A.add)
-        copy(R("el", 16, 16 * t), R("e3", 16, 16 * t))
+            y, q, p = 144 * k, 16 * t + 8 * h, R("pb7", 8, 256)
+            mm(p, [(R("Y", 128, y + 15 - s), ("ID", s, 128, 16)) for s in range(16)], tag="elist")
+            ts(R("e1", 8, q), p, 0.0, A.is_equal, 1024.0, A.mult)
+            tt(R("e2", 8, q), p, R("LT", 8, 8 * h), A.add)
+            tt(R("e3", 8, q), R("e2", 8, q), R("e1", 8, q), A.add)
+            copy(R("el", 8, q), R("e3", 8, q))
 
     hot[0] = HOT
     for e in range(4):
@@ -330,24 +344,25 @@ def build():
     chain(5)
     for e in range(4):
         for c in range(NCH):
+            hot[0] = -CO[0][c]
             trial(0, e, c)
+    hot[0] = 0.0
     prices(0)
     for c in range(NCH):
         r = lambda b, k=0: R(b, CW, k + CW * c)
         n = 16 * CW
-        gath("s", R("x", n, n * c), R("P0", W), r("T16"), tag="x04%d" % c)
+        gath(R("x", n, n * c), R("P0", W), r("T16"), tag="x04%d" % c)
         add("v", vc(n, 0.5), lambda g, T, X, c=c, n=n: g.vector.tensor_tensor_scan(T["sm"][:, n * c:n * c + n], T["scd"][:, 0:n], T["x"][:, n * c:n * c + n], 0.0, A.mult, A.max),
             [R("scd", n), R("x", n, n * c)], [R("sm", n, n * c)], tag="scan")
         mm(R("pb7", CW), [(R("BDw", 128), ("sm", n * c + 15, n * c + n, 16))], tag="u")
-        ts(r("Q"), r("Lr"), 32.0, A.mult, 2464.0, A.add)
         ts(r("w1"), R("pb7", CW), 2.0, A.mult, 1.0, A.add)
         ts(r("w2"), r("w1"), 2047, A.bitwise_and)
-        tt(r("w3"), r("w2"), r("Lr"), A.mult)
-        tt(r("w4"), r("w3"), r("Q"), A.add)
+        ts(r("Q"), r("w2"), 32.0, A.add)
+        tt(r("w3"), r("Q"), r("Lr"), A.mult)
+        ts(r("w4"), r("w3"), 2464.0, A.add)
         ts(r("w5"), r("w4"), 5, A.logical_shift_right, 2047, A.bitwise_and)
         copy(r("T16", L), r("w5"))
         ts(r("TT", L), r("w5"), float(OFFS), A.add)
-        copy(r("A16", 4 * L), r("Lr"))
         copy(r("yhf"), r("Lr"))
         act(r("AC", 4 * L), r("yhf"), con[0])
     dma(lambda T: T.yh[:, 0:L], lambda T: T["yhf"][:, 0:L], 128, [R("yhf", L)], [])
@@ -357,20 +372,21 @@ def build():
     claim_forms(4, 1)
     parents(0)
     for e in (1, 2, 3):
-        gath("s", R("Bf", L, L * e), R("Btab", 4 * L, 512 + L * (e - 1)), R("el", 16))
+        gath(R("Bf", L, L * e), R("Btab", 4 * L, 512 + L * (e - 1)), R("el", 16))
         lot_forms(4 + e, R("Bf", L, L * e), e)
     hot[0] = -HOT
     for j in range(3):
-        gath("s", R("ctab", L, L * (j + 1)), R("btab", 4 * L, L * j), R("el", 16))
+        gath(R("ctab", L, L * (j + 1)), R("btab", 4 * L, L * j), R("el", 16))
     dma(lambda T: T.yv[:, 0:L], lambda T: T["ctab"][0::16, L:2 * L], 8, [R("ctab", L, L)], [])
     hot[0] = HOT
     for e in range(4):
         trial(1, e, None)
     claims(1)
-    hot[0] = 0.0
     for e in range(4):
         for c in range(NCH):
+            hot[0] = -CO[1][c]
             trial(1, e, c)
+    hot[0] = 0.0
     prices(1)
     for c in range(NCH):
         copy(R("yhf", CW, L + CW * c), R("Lr", CW, L + CW * c))
@@ -378,8 +394,9 @@ def build():
             o = L + 128 * (c // 2)
             dma(lambda T, o=o: T.yh[:, o:o + 128], lambda T, o=o: T["yhf"][:, o:o + 128], 64, [R("yhf", 128, o)], [])
     parents(1)
-    gath("s", R("par", L), R("ctab", 4 * L), R("el", 16, 16))
-    dma(lambda T: T.yv[:, L:2 * L], lambda T: T["par"][0::16, :], 8, [R("par", L)], [])
+    for h in range(2):
+        gath(R("par", 128, 128 * h), R("ctab", 4 * L), R("el", 8, 16 + 8 * h))
+        dma(lambda T, h=h: T.yv[:, L + 128 * h:L + 128 * h + 128], lambda T, h=h: T["par"][0::16, 128 * h:128 * h + 128], 4, [R("par", 128, 128 * h)], [])
     return ops
 
 
@@ -412,7 +429,7 @@ def schedule(ops, deps):
     lev = [0.0] * n
     for i in range(n - 1, -1, -1):
         lev[i] = ops[i]["cost"] + max([lev[k] + LAT for k in succ[i]] or [0.0])
-    wgt = [lev[i] + ops[i]["hot"] for i in range(n)]
+    wgt = [lev[i] + ops[i]["hot"] + JIT * ((i + 1) * MIX % 1009) / 1009.0 for i in range(n)]
     left = [len(d) for d in deps]
     ready = [0.0] * n
     cand, free, order = {}, {}, []
@@ -429,7 +446,7 @@ def schedule(ops, deps):
         if best is None:
             break
         t, q = best
-        i = max((i for i in cand[q] if ready[i] <= t + (DH if ops[i]["hot"] > 0 else DM) + 1e-9), key=lambda i: (wgt[i], -i))
+        i = max((i for i in cand[q] if ready[i] <= t + (DH if ops[i]["hot"] > 100 else DM) + 1e-9), key=lambda i: (wgt[i], -i))
         t = max(t, ready[i])
         cand[q].remove(i)
         o = ops[i]
@@ -473,8 +490,9 @@ def routes(cores, topo):
     return out
 
 
-def slot(cores, src, dst):
-    return [c for c in cores if c != dst].index(src)
+def slot(cores, src, dst, topo):
+    rest = [c for c in cores if c != dst]
+    return sorted(rest, key=lambda c: (not topo.same_plane(c, dst), c)).index(src)
 
 
 def bits(es):
@@ -494,13 +512,13 @@ def hand_on(g, core, T, topo):
                 continue
             es, into = topo.engines(core, d), onchip(c, peers, topo, h)
             rid, pid = topo.addr(d, core)
-            k = slot(cores, c, d)
+            k = slot(cores, c, d, topo)
             for t in range(2):
                 for b in range(NB):
                     g.wait_ge(T.sem["hin%d_%d" % (t, b)], len(into))
                     o = k * W + BW * b
                     g.remote_dma(T["LO%d" % t][:, o:o + BW], T["HB"][:, t * W + BW * b:t * W + BW * b + BW],
-                                 T.sem["arr%d_%d" % (t, b)], T.sem["hs"], pid, rid, bits(es))
+                                 T.sem["far%d_%d" % (t, b)], T.sem["hs"], pid, rid, bits(es))
             g.wait_ge(T.sem["hs"], 2 * NB * len(es))
 
 
@@ -519,7 +537,7 @@ def rank_program(g, core, T, topo):
         p, hs = peers[0], list(hop.values())
         src = T["O%d" % t][:, BW * b:BW * b + BW]
         dst = lambda h: DstId(rid=topo.addr(h, core)[0], pnc=topo.addr(h, core)[1])
-        k = slot(cores, core, p) * W + BW * b
+        k = slot(cores, core, p, topo) * W + BW * b
         e0, e1 = topo.engines(core, p), onchip(core, peers, topo, hs[0])
         g.remote_dma_fused([
             RemoteDMATransfer(dst_ids=[dst(p)], dma_engine_mask=bits(e0), remote_sem=T.sem["arr%d_%d" % (t, b)],
@@ -529,7 +547,7 @@ def rank_program(g, core, T, topo):
             local_sem=T.sem["snd"])
         sent[0] += len(e0) + len(e1)
 
-    arrive = len(topo.engines(peers[0], core)) + sum(len(topo.engines(h[core], core)) for _, h in rt if core in h)
+    arrive = {"a": len(topo.engines(peers[0], core)), "f": sum(len(topo.engines(h[core], core)) for _, h in rt if core in h)}
     X = {"send": send}
     cnt = {"v": 0, "s": 0, "t": 0, "g": 0}
     clock = {q: {} for q in eng}
@@ -539,7 +557,8 @@ def rank_program(g, core, T, topo):
     for i in order:
         o = ops[i]
         if o["kind"] == "x":
-            done[i] = (o["fn"], arrive, {o["fn"]: arrive})
+            n = arrive[o["fn"][0]]
+            done[i] = (o["fn"], n, {o["fn"]: n})
             continue
         q = o["q"]
         ck = clock[q]

from concourse.bass import DstId, RemoteDMATransfer
from concourse.mybir import AluOpType, ActivationFunctionType

OFFS, BIG = 131072, 16384
W, L, H0 = 2048, 256, 768
NCH, CW = 4, 64
NB = 2
BW = W // NB
BF, F32, I32, U16, F16 = "bfloat16", "float32", "int32", "uint16", "float16"
CYC = 0.83e-3 * 1.2
LAT, HOT, XT, XT1, FP = 0.1, 500.0, 14.0, 14.0, 0.6
DH, DM = 0.1, 0.05
SMH, JIT, MIX = 2.0, 0.3, 933
CO = ((0, 0, 0, 0), (0, -1.6, 0, 0))
SPLIT = 2

SCRATCH = {
    "P0": ("sbuf", [128, W], BF), "P1": ("sbuf", [128, W], BF), "P2": ("sbuf", [128, W], BF),
    "ps0": ("sbuf", [128, W], BF), "ps1": ("sbuf", [128, W], BF),
    "pk": ("sbuf", [128, H0], I32), "pv": ("sbuf", [128, H0], I32), "lt": ("sbuf", [128, L], I32),
    "lc": ("sbuf", [128, 16], I32), "ac": ("sbuf", [128, 16], I32),
    "ic": ("sbuf", [128, 1], I32), "wc": ("sbuf", [128, 1], I32), "sc": ("sbuf", [128, 2], I32),
    "icf": ("sbuf", [128, 1], F32), "wcf": ("sbuf", [128, 1], F32), "scf": ("sbuf", [128, 2], F32), "mo": ("sbuf", [128, 1], F32),
    "ip": ("sbuf", [128, 1], I32), "im": ("sbuf", [128, 128], I32), "on": ("sbuf", [128, W], BF),
    "pg": ("sbuf", [128, 1], I32), "pgf": ("sbuf", [128, 1], F32), "pg16": ("sbuf", [128, 1], F32), "ipf": ("sbuf", [128, 1], F32),
    "pl": ("sbuf", [128, 1], I32), "plf": ("sbuf", [128, 1], F32), "mg": ("sbuf", [128, 128], I32),
    "Z": ("sbuf", [128, 144], BF), "Zh": ("sbuf", [128, 144], F16), "BR": ("sbuf", [128, 128], F16),
    "BDw": ("sbuf", [128, 128], BF), "IB": ("sbuf", [128, 128], BF), "IL": ("sbuf", [128, 128], BF),
    "ID": ("sbuf", [128, 128], BF), "DG": ("sbuf", [128, 128], BF), "E": ("sbuf", [128, W], BF),
    "scd": ("sbuf", [128, 1024], BF), "LT": ("sbuf", [128, 16], F32),
    "pvh": ("sbuf", [128, H0], F16), "vt": ("sbuf", [128, H0], F32), "btab": ("sbuf", [128, 6 * L], F32),
    "Btab": ("sbuf", [128, 512 + 6 * L], F32), "bh": ("sbuf", [128, 6 * L], F16), "lst": ("sbuf", [128, 6 * 16], U16),
    "A16": ("sbuf", [128, 8 * L], U16), "AC": ("sbuf", [128, 8 * L], F32), "Bf": ("sbuf", [128, 4 * L], F32),
    "A16c": ("sbuf", [128, 8 * 16], U16), "ACc": ("sbuf", [128, 8 * 16], F32),
    "T16": ("sbuf", [128, 2 * L], U16), "TT": ("sbuf", [128, 2 * L], I32), "Lr": ("sbuf", [128, 2 * L], I32),
    "T16c": ("sbuf", [128, 32], U16), "TTc": ("sbuf", [128, 32], I32), "Lc": ("sbuf", [128, 16], I32),
    "x": ("sbuf", [128, 4096 + 256], BF), "mk": ("sbuf", [128, 4096 + 256], BF), "sm": ("sbuf", [128, 4096], BF),
    "yhf": ("sbuf", [128, 2 * L], F32), "Q": ("sbuf", [128, L], I32),
    "w1": ("sbuf", [128, L], I32), "w2": ("sbuf", [128, L], I32), "w3": ("sbuf", [128, L], I32), "w4": ("sbuf", [128, L], I32),
    "w5": ("sbuf", [128, L], I32),
    "hi": ("sbuf", [128, 2 * L], I32), "hb": ("sbuf", [128, 2 * L], BF), "hm": ("sbuf", [128, 512], BF),
    "Y": ("sbuf", [128, 4 * 144], BF), "e1": ("sbuf", [128, 32], F32), "e2": ("sbuf", [128, 32], F32), "e3": ("sbuf", [128, 32], F32),
    "el": ("sbuf", [128, 32], U16), "ctab": ("sbuf", [128, 4 * L], F32), "par": ("sbuf", [128, L], F32),
    "hl": ("sbuf", [128, 64], I32), "hlb": ("sbuf", [128, 64], F32),
    "OH": ("sbuf", [128, 16 * 128], BF), "OL": ("sbuf", [128, 16 * 128], BF), "C": ("sbuf", [128, 256], BF),
    "O0": ("sbuf", [128, W], BF), "O1": ("sbuf", [128, W], BF), "N16": ("sbuf", [128, W], F16),
    "LO0": ("sbuf", [128, 3 * W], BF), "LO1": ("sbuf", [128, 3 * W], BF),
    "HB": ("sbuf", [128, 2 * W], BF),
}
for _i in range(8):
    SCRATCH["pb%d" % _i] = ("psum", [128, 512], F32)
ND = 48
SEMAPHORES = ["qv", "qs", "qt", "qg", "snd", "hs"] + ["d%d" % i for i in range(ND)] + \
    ["%s%d_%d" % (n, t, b) for n in ("arr", "far", "hin") for t in range(2) for b in range(NB)]

A = AluOpType
AF = ActivationFunctionType


def build():
    ops = []
    hot = [0.0]

    def add(q, cost, fn, rd, wr, kind="c", tag=""):
        ops.append({"q": q, "cost": cost, "fn": fn, "rd": rd, "wr": wr, "kind": kind, "tag": tag, "hot": hot[0]})

    def vc(n, cyc=1.0):
        return max(64, n * cyc) * CYC + 0.01

    def ga(n):
        return n * 1.55 * CYC + 0.06

    def S(T, r):
        return T[r[0]][:, r[1]:r[2]] if len(r) == 3 else T[r[0]][:, r[1]:r[2]:r[3]]

    def n_of(r):
        return len(range(*r[1:]))

    def copy(out, in_, cyc=1.0, tag=""):
        add("v", vc(n_of(out), cyc), lambda g, T, X: g.vector.tensor_copy(S(T, out), S(T, in_)), [in_], [out], tag=tag)

    def ts(out, in_, s1, op0, s2=None, op1=None, cyc=1.0, tag=""):
        rd = [in_] + [s for s in (s1, s2) if isinstance(s, tuple)]

        def fn(g, T, X):
            a = S(T, s1) if isinstance(s1, tuple) else s1
            b = S(T, s2) if isinstance(s2, tuple) else s2
            if op1 is None:
                return g.vector.tensor_scalar(S(T, out), S(T, in_), a, None, op0)
            return g.vector.tensor_scalar(S(T, out), S(T, in_), a, b, op0, op1)
        add("v", vc(n_of(out), cyc), fn, rd, [out], tag=tag)

    def tt(out, a, b, op, tag=""):
        two = 1.0 if (a[0][:2] == "pb" or b[0][:2] == "pb") else 2.0
        add("v", vc(n_of(out), two), lambda g, T, X: g.vector.tensor_tensor(S(T, out), S(T, a), S(T, b), op), [a, b], [out], tag=tag)

    def act(out, in_, bias=0.0, tag=""):
        def fn(g, T, X):
            if bias:
                return g.scalar.activation(S(T, out), S(T, in_), AF.Copy, bias=bias)
            return g.scalar.activation(S(T, out), S(T, in_), AF.Copy)
        add("s", n_of(out) * CYC + 0.06, fn, [in_], [out], tag=tag)

    def relu(out, in_, bias, scale, tag=""):
        add("s", n_of(out) * CYC + 0.06, lambda g, T, X: g.scalar.activation(S(T, out), S(T, in_), AF.Relu, bias=S(T, bias), scale=scale),
            [in_, bias], [out], tag=tag)

    def gath(out, win, off, tag="", comp=False):
        def fn(g, T, X):
            i = S(T, win).indirect(S(T, off))
            if comp:
                return g.scalar.activation(S(T, out), i, AF.Copy, bias=255.0, scale=-1.0)
            return g.scalar.activation(S(T, out), i, AF.Copy)
        add("s", ga(n_of(out)), fn, [win, off], [out], tag=tag)

    def mm(out, pairs, tag="", k=128, first=True, last=True):
        def fn(g, T, X):
            r = None
            for i, (l, h) in enumerate(pairs):
                a, b = (S(T, l), S(T, h)) if k == 128 else (T[l[0]][0:k, l[1]:l[2]], T[h[0]][0:k, h[1]:h[2]])
                r = g.tensor.matmul(S(T, out), a, b, first and i == 0, last and i == len(pairs) - 1)
            return r
        add("t", sum(max(64, n_of(h)) for l, h in pairs) * CYC + 0.06, fn, [p for lh in pairs for p in lh], [out], tag=tag)

    def dma(out, in_, kb, rd, wr, q="y", tag=""):
        def fn(g, T, X):
            return (g.sync if q == "y" else g.scalar).dma_start(out(T), in_(T))
        add(q, 2.0 + kb / 180.0, fn, rd, wr, kind="d", tag=tag)

    def iota(out, pattern, base, cm, small=False):
        n = n_of(out)

        def fn(g, T, X):
            if small:
                return g.iota(S(T, out), pattern, base, cm, allow_small_or_imprecise_dtypes=True)
            return g.iota(S(T, out), pattern, base, cm)
        add("g", 0.15 + 2 * n * CYC, fn, [], [out])

    def select(out, in_, pattern, cmp, cm):
        add("g", 0.17 + 2 * n_of(out) * CYC, lambda g, T, X: g.affine_select(S(T, out), S(T, in_), pattern, cmp, 0.0, 0, cm), [in_], [out])

    def mset(out, v):
        add("v", vc(n_of(out), 0.5), lambda g, T, X: g.vector.memset(S(T, out), v), [], [out])

    R = lambda b, n, a=0: (b, a, a + n)

    hot[0] = 2000.0
    dma(lambda T: T["pv"][0:8, :], lambda T: T.prev[:], 24, [], [R("pv", H0)], q="s")
    hot[0] = 1990.0
    dma(lambda T: T["lc"][:], lambda T: T.lots[0::16, :], 8, [], [R("lc", 16)])
    hot[0] = 1985.0
    dma(lambda T: T["P0"][:, 0:W], lambda T: T.price[:], 512, [], [R("P0", W)], q="s")
    hot[0] = 1980.0
    dma(lambda T: T["sc"][:], lambda T: T.slack[:], 1, [], [R("sc", 2)])
    dma(lambda T: T["ac"][:], lambda T: T.packs[0::16, H0 - L:H0], 8, [], [R("ac", 16)])
    dma(lambda T: T["lt"][:], lambda T: T.lots[:], 128, [], [R("lt", L)])
    hot[0] = 1970.0
    dma(lambda T: T["pk"][:], lambda T: T.packs[:], 384, [], [R("pk", H0)])
    hot[0] = 0.0
    dma(lambda T: T["wc"][:], lambda T: T.wt[:], 1, [], [R("wc", 1)])
    dma(lambda T: T["ic"][:], lambda T: T.inc[:], 1, [], [R("ic", 1)])
    iota(R("ip", 1), [[1, 1]], 0, 1)
    iota(R("im", 128), [[1, 128]], 0, 0)
    iota(R("btab", L), [[1, L]], H0 - L, 0, True)
    iota(R("IL", 128), [[1, 128]], 0, 0, True)
    iota(R("on", W), [[0, W]], 1, 0, True)
    select(R("ID", 128), R("on", 128), [[-1, 128]], A.is_equal, 1)
    select(R("scd", 1024), R("on", 1024), [[0, 64], [1, 16]], A.not_equal, 0)
    select(R("E", W), R("on", W), [[-1, 16], [-16, 8], [0, 16]], A.is_equal, 1)
    hot[0] = -HOT
    iota(R("ctab", L), [[1, L]], H0, 0, True)
    hot[0] = HOT
    mset(R("Z", 144), 0.0)
    ts(R("pg", 1), R("ip", 1), 4, A.logical_shift_right)
    copy(R("ipf", 1), R("ip", 1))
    copy(R("pgf", 1), R("pg", 1))
    ts(R("mg", 128), R("im", 128), 4, A.logical_shift_right)
    ts(("Z", 15, 128, 16), R("im", 8), R("pgf", 1), A.is_equal, float(BIG), A.mult)
    ts(R("BR", 128), R("mg", 128), R("ipf", 1), A.is_equal)
    ts(R("Zh", 144), R("Z", 144), 1.0 / BIG, A.mult)
    hot[0] = 0.0
    mset(R("mo", 1), -256.0)
    ts(R("pg16", 1), R("pg", 1), 16.0, A.mult)
    ts(R("IB", 128), R("im", 128), R("pg16", 1), A.subtract)
    ts(R("icf", 1), R("ic", 1), 1.0 / 64, A.mult)
    ts(R("DG", 128), R("im", 128), R("ipf", 1), A.is_equal, R("icf", 1), A.mult)
    copy(R("wcf", 1), R("wc", 1))
    ts(R("BDw", 128), R("mg", 128), R("pgf", 1), A.is_equal, R("wcf", 1), A.mult)
    ts(R("pl", 1), R("ip", 1), 15, A.bitwise_and)
    copy(R("plf", 1), R("pl", 1))
    ts(R("LT", 16), R("im", 16), 16.0, A.mult, R("plf", 1), A.add)
    ts(R("LT", 16), R("LT", 16), -256.0, A.add)
    mset(R("Y", 576), 0.0)
    con = [float(2048 * (e + 1) + OFFS) for e in range(4)]
    hot[0] = 4 * HOT
    copy(R("T16c", 16), R("lc", 16))
    hot[0] = 3 * HOT
    copy(R("A16c", 16), R("ac", 16))
    ts(R("scf", 2), R("sc", 2), -1.0, A.mult, 255.0, A.add)
    relu(R("ps0", W), R("P0", W), R("scf", 1), -1.0, tag="ps0")
    ts(R("ACc", 16), R("ac", 16), con[0], A.add)
    ts(R("TTc", 16), R("lc", 16), float(OFFS), A.add)
    hot[0] = HOT
    for o, n in ((512, 256), (0, 512)):
        add("v", vc(n), lambda g, T, X, o=o, n=n: g.vector.tensor_copy(T["pvh"][0:8, o:o + n], T["pv"][0:8, o:o + n]), [R("pv", n, o)], [R("pvh", n, o)])
    mm(R("pb1", 256), [(R("BR", 128), R("pvh", 256, 512))], k=8)
    mm(R("pb0", 512), [(R("BR", 128), R("pvh", 512))], k=8)
    copy(R("bh", L, L), R("pb1", 256))
    act(R("vt", 256, 512), R("pb1", 256))
    act(R("vt", 512), R("pb0", 512))
    hot[0] = 2 * HOT
    copy(R("T16", L), R("lt", L))
    copy(R("A16", L), R("pk", L, H0 - L))
    hot[0] = HOT
    copy(R("Btab", H0), R("pk", H0))
    hot[0] = 0.0
    ts(R("TT", L), R("lt", L), float(OFFS), A.add)
    act(R("AC", L), R("Btab", L, 512), con[0])
    hot[0] = -HOT
    act(R("btab", L, L), R("vt", L, 512))

    def lot_forms(i, src, e):
        copy(R("A16", L, L * i), src, tag="A16")
        act(R("AC", L, L * i), src, con[e], tag="AC")
        claim_forms(i, i // 4)

    def claim_forms(i, t):
        src, a = ("T16", 0) if i == 4 else ("A16", L * i)
        dma(lambda T: T["A16c"][:, 16 * i:16 * i + 16], lambda T: T[src][t::16, a:a + L], 8, [R(src, L, a)], [R("A16c", 16, 16 * i)])
        dma(lambda T: T["ACc"][:, 16 * i:16 * i + 16], lambda T: T["AC"][t::16, L * i:L * i + L], 8, [R("AC", L, L * i)], [R("ACc", 16, 16 * i)])

    def chain(e):
        hot[0] = HOT if e < 4 else 0.0
        mm(R("pb7", 16), [(R("Zh", 128, 15 - s), ("bh", L * e + s, L * e + L, 16)) for s in range(16)], tag="list")
        ts(R("lst", 16, 16 * e), R("pb7", 16), 1.0 / 16, A.mult)
        if e < 5:
            gath(R("btab", L, L * (e + 1)), R("vt", H0), R("lst", 16, 16 * e))
            copy(R("bh", L, L * (e + 1)), R("btab", L, L * (e + 1)))
        gath(R("Btab", L, 512 + L * e), R("Btab", H0), R("lst", 16, 16 * e))
        if e < 4:
            lot_forms(e, R("Btab", L, 512 + L * e), e)
        hot[0] = 0.0

    for e in range(1, 4):
        chain(e)

    def trial(t, e, c):
        i = 4 * t + e
        if c is None:
            w, xo, pb, parts = 16, 4096, "pb6", 1
            a16, acd, t16, tcd, l = R("A16c", 16, 16 * i), R("ACc", 16, 16 * i), R("T16c", 16, 16 * t), R("TTc", 16, 16 * t), R("Lc", 16)
        else:
            w, xo, pb, parts = CW, 16 * CW * c, "pb%d" % (2 + c % 4), SPLIT
            a16, acd = R("A16", w, L * i + w * c) if i != 4 else R("T16", w, w * c), R("AC", w, L * i + w * c)
            t16, tcd, l = R("T16", w, L * t + w * c), R("TT", w, L * t + w * c), R("Lr", w, L * t + w * c)
        n, ps = 16 * w, "ps%d" % t
        tag = "t%d%d%s" % (t, e, c)
        for s in range(parts):
            nn, ww = n // parts, w // parts
            xs, ts_, as_ = R("x", nn, xo + nn * s), R(t16[0], ww, t16[1] + ww * s), R(a16[0], ww, a16[1] + ww * s)
            gath(xs, R("P%d" % t, W), ts_, tag="x" + tag, comp=True)
            add("v", ga(nn), lambda g, T, X, xs=xs, as_=as_: g.vector.tensor_tensor(T["mk"][:, xs[1]:xs[2]], T[ps][:, 0:W].indirect(S(T, as_)), S(T, xs), A.is_gt),
                [R(ps, W), as_, xs], [("mk", xs[1], xs[2])], tag="m" + tag)
        mm(R(pb, w), [(R("Z", 128, 15 - k), ("mk", xo + k, xo + n, 16)) for k in range(16)], tag="c" + tag)
        h0 = hot[0]
        hot[0] += SMH if c is not None else 0.0
        tt(R(pb, w, 128), R(pb, w), acd, A.min)
        tt(tcd, R(pb, w, 128), tcd, A.max)
        if c is not None or e < 3:
            ts(l, tcd, 2047, A.bitwise_and)
        if e < 3 or (t == 0 and c is not None):
            copy(t16, l)
        hot[0] = h0

    def claims(t):
        P, O, LO = "P%d" % t, "O%d" % t, "LO%d" % t
        ts(R("hl", 16, 32 * t), R("TTc", 16, 16 * t), 7, A.logical_shift_right, 15, A.bitwise_and)
        ts(R("hl", 16, 32 * t + 16), R("TTc", 16, 16 * t), 127, A.bitwise_and)
        copy(R("hlb", 32, 32 * t), R("hl", 32, 32 * t))
        for s in range(16):
            ts(R("OH", 128, 128 * s), R("IB", 128), R("hlb", 1, 32 * t + s), A.is_equal, cyc=0.5)
            ts(R("OL", 128, 128 * s), R("IL", 128), R("hlb", 1, 32 * t + 16 + s), A.is_equal, cyc=0.5)
        mm(R("pb7", 128), [(R("OH", 128, 128 * s), R("OL", 128, 128 * s)) for s in range(16)], tag="C%d" % t)
        if t == 0:
            ts(R("C", 128), R("pb7", 128), 1.0, A.min, 256.0, A.mult)
        else:
            ts(R("C", 128, 128), R("pb7", 128), 1.0, A.min)
        for b in range(4):
            pb, o = "pb%d" % (b % 2), 512 * b

            def fn(g, T, X, o=o, pb=pb):
                r = None
                for h in range(0, 512, 128):
                    if t == 0:
                        g.tensor.matmul(T[pb][:, h:h + 128], T["ID"][:], T[P][:, o + h:o + h + 128], True, False)
                    r = g.tensor.matmul(T[pb][:, h:h + 128], T["E"][:, o + h:o + h + 128], T["C"][:, 128 * t:128 * t + 128], t == 1, True)
                return r
            add("t", 512 * CYC * (2 - t), fn, [R("ID", 128), R(P, 512, o), R("E", 512, o), R("C", 128, 128 * t)], [R(pb, 512)], tag="F")
            if t == 0:
                relu(R(O, 512, o), R(pb, 512), R("mo", 1), 1.0, tag="O")
            else:
                tt(R(O, 512, o), R(pb, 512), R(P, 512, o), A.mult, tag="O")
            if (b + 1) * 512 % BW == 0:
                k = ((b + 1) * 512 - 1) // BW
                add("g", 1.0, lambda g, T, X, k=k: X["send"](g, T, t, k), [R(O, BW, BW * k)], [("wire%d" % t, k, k + 1)], kind="r", tag="send")
                for far in (0, 1):
                    add("x%d%d%d" % (far, t, k), ((XT, XT1)[t] + 3.0 * k) * (FP, 1.0)[far], "%s%d_%d" % (("arr", "far")[far], t, k), [("wire%d" % t, k, k + 1)],
                        [R(LO, BW, q * W + BW * k) for q in ((0,), (1, 2))[far]], kind="x", tag="arrive")

    def prices(t):
        P, N, LO = "P%d" % t, "P%d" % (t + 1), "LO%d" % t
        for b in range(4):
            o, pb = 512 * b, "pb%d" % (b % 2)
            mm(R(pb, 512), [(R("ID", 128), R(P, 512, o)), (R("DG", 128), R(LO, 512, o))], tag="W1", last=False)
            mm(R(pb, 512), [(R("DG", 128), R(LO, 512, q * W + o)) for q in (1, 2)], tag="W2", first=False)
            ts(R("N16", 512, o), R(pb, 512), 1025.0 - 63.0 / 128, A.add, 1280.0, A.min)
            ts(R(N, 512, o), R("N16", 512, o), -1025.0, A.add, cyc=0.5)
            if t == 0:
                relu(R("ps1", 512, o), R(N, 512, o), R("scf", 1, 1), -1.0, tag="ps1")
            else:
                dma(lambda T, o=o: T.yp[:, o:o + 512], lambda T, o=o: T["P2"][:, o:o + 512], 128, [R("P2", 512, o)], [], q="ys"[b % 2])

    def parents(t):
        for h in range(2):
            o, k = L * t + 128 * h, 2 * t + h
            ts(R("hi", 128, o), R("TT", 128, o), 11, A.logical_shift_right, 7, A.bitwise_and)
            copy(R("hb", 128, o), R("hi", 128, o))
            mm(R("pb7", 128), [(R("hb", 128, o), R("ID", 128))], tag="hT")
            add("v", vc(128), lambda g, T, X, k=k: g.vector.tensor_tensor_scan(T["hm"][:, 128 * k:128 * k + 128], T["scd"][:, 0:128], T["pb7"][:, 0:128], 0.0, A.mult, A.max),
                [R("scd", 128), R("pb7", 128)], [R("hm", 128, 128 * k)])
            ts(("Y", 144 * k + 15, 144 * k + 128, 16), ("hm", 128 * k + 15, 128 * k + 128, 16), 256.0, A.mult)
            y, q, p = 144 * k, 16 * t + 8 * h, R("pb7", 8, 256)
            mm(p, [(R("Y", 128, y + 15 - s), ("ID", s, 128, 16)) for s in range(16)], tag="elist")
            ts(R("e1", 8, q), p, 0.0, A.is_equal, 1024.0, A.mult)
            tt(R("e2", 8, q), p, R("LT", 8, 8 * h), A.add)
            tt(R("e3", 8, q), R("e2", 8, q), R("e1", 8, q), A.add)
            copy(R("el", 8, q), R("e3", 8, q))

    hot[0] = HOT
    for e in range(4):
        trial(0, e, None)
    claims(0)
    chain(4)
    chain(5)
    for e in range(4):
        for c in range(NCH):
            hot[0] = -CO[0][c]
            trial(0, e, c)
    hot[0] = 0.0
    prices(0)
    for c in range(NCH):
        r = lambda b, k=0: R(b, CW, k + CW * c)
        n = 16 * CW
        gath(R("x", n, n * c), R("P0", W), r("T16"), tag="x04%d" % c)
        add("v", vc(n, 0.5), lambda g, T, X, c=c, n=n: g.vector.tensor_tensor_scan(T["sm"][:, n * c:n * c + n], T["scd"][:, 0:n], T["x"][:, n * c:n * c + n], 0.0, A.mult, A.max),
            [R("scd", n), R("x", n, n * c)], [R("sm", n, n * c)], tag="scan")
        mm(R("pb7", CW), [(R("BDw", 128), ("sm", n * c + 15, n * c + n, 16))], tag="u")
        ts(r("w1"), R("pb7", CW), 2.0, A.mult, 1.0, A.add)
        ts(r("w2"), r("w1"), 2047, A.bitwise_and)
        ts(r("Q"), r("w2"), 32.0, A.add)
        tt(r("w3"), r("Q"), r("Lr"), A.mult)
        ts(r("w4"), r("w3"), 2464.0, A.add)
        ts(r("w5"), r("w4"), 5, A.logical_shift_right, 2047, A.bitwise_and)
        copy(r("T16", L), r("w5"))
        ts(r("TT", L), r("w5"), float(OFFS), A.add)
        copy(r("yhf"), r("Lr"))
        act(r("AC", 4 * L), r("yhf"), con[0])
    dma(lambda T: T.yh[:, 0:L], lambda T: T["yhf"][:, 0:L], 128, [R("yhf", L)], [])
    hot[0] = HOT / 2
    dma(lambda T: T["T16c"][:, 16:32], lambda T: T["T16"][1::16, L:2 * L], 8, [R("T16", L, L)], [R("T16c", 16, 16)])
    dma(lambda T: T["TTc"][:, 16:32], lambda T: T["TT"][1::16, L:2 * L], 8, [R("TT", L, L)], [R("TTc", 16, 16)])
    claim_forms(4, 1)
    parents(0)
    for e in (1, 2, 3):
        gath(R("Bf", L, L * e), R("Btab", 4 * L, 512 + L * (e - 1)), R("el", 16))
        lot_forms(4 + e, R("Bf", L, L * e), e)
    hot[0] = -HOT
    for j in range(3):
        gath(R("ctab", L, L * (j + 1)), R("btab", 4 * L, L * j), R("el", 16))
    dma(lambda T: T.yv[:, 0:L], lambda T: T["ctab"][0::16, L:2 * L], 8, [R("ctab", L, L)], [])
    hot[0] = HOT
    for e in range(4):
        trial(1, e, None)
    claims(1)
    for e in range(4):
        for c in range(NCH):
            hot[0] = -CO[1][c]
            trial(1, e, c)
    hot[0] = 0.0
    prices(1)
    for c in range(NCH):
        copy(R("yhf", CW, L + CW * c), R("Lr", CW, L + CW * c))
        if c % 2:
            o = L + 128 * (c // 2)
            dma(lambda T, o=o: T.yh[:, o:o + 128], lambda T, o=o: T["yhf"][:, o:o + 128], 64, [R("yhf", 128, o)], [])
    parents(1)
    for h in range(2):
        gath(R("par", 128, 128 * h), R("ctab", 4 * L), R("el", 8, 16 + 8 * h))
        dma(lambda T, h=h: T.yv[:, L + 128 * h:L + 128 * h + 128], lambda T, h=h: T["par"][0::16, 128 * h:128 * h + 128], 4, [R("par", 128, 128 * h)], [])
    return ops


def depend(ops):
    acc, deps = {}, []
    for i, o in enumerate(ops):
        d = set()
        for wr, rs in ((False, o["rd"]), (True, o["wr"])):
            for r in rs:
                for (j, a, b, w) in acc.get(r[0], []):
                    bank = r[0][:2] == "pb" and ops[j]["q"] != o["q"]
                    if j != i and (bank or ((w or wr) and a < r[2] and r[1] < b)):
                        d.add(j)
        for wr, rs in ((False, o["rd"]), (True, o["wr"])):
            for r in rs:
                lst = acc.setdefault(r[0], [])
                if wr and r[0][:2] != "pb" and len(r) == 3:
                    lst[:] = [e for e in lst if not (r[1] <= e[1] and e[2] <= r[2] and e[0] in d)]
                lst.append((i, r[1], r[2], wr))
        deps.append(sorted(d))
    return deps


def schedule(ops, deps):
    n = len(ops)
    succ = [[] for _ in range(n)]
    for i, d in enumerate(deps):
        for j in d:
            succ[j].append(i)
    lev = [0.0] * n
    for i in range(n - 1, -1, -1):
        lev[i] = ops[i]["cost"] + max([lev[k] + LAT for k in succ[i]] or [0.0])
    wgt = [lev[i] + ops[i]["hot"] + JIT * ((i + 1) * MIX % 1009) / 1009.0 for i in range(n)]
    left = [len(d) for d in deps]
    ready = [0.0] * n
    cand, free, order = {}, {}, []
    for i in range(n):
        if not left[i]:
            cand.setdefault(ops[i]["q"], []).append(i)
    while True:
        best = None
        for q, l in cand.items():
            if l:
                t = max(free.get(q, 0.0), min(ready[i] for i in l))
                if best is None or t < best[0]:
                    best = (t, q)
        if best is None:
            break
        t, q = best
        i = max((i for i in cand[q] if ready[i] <= t + (DH if ops[i]["hot"] > 100 else DM) + 1e-9), key=lambda i: (wgt[i], -i))
        t = max(t, ready[i])
        cand[q].remove(i)
        o = ops[i]
        fin = t + o["cost"]
        if o["kind"] == "d":
            free["dma"] = max(free.get("dma", 0.0), t) + o["cost"] - 2.0
            fin = free["dma"] + 2.0
        free[q] = t + (0.1 if o["kind"] == "d" else o["cost"])
        order.append(i)
        for k in succ[i]:
            left[k] -= 1
            ready[k] = max(ready[k], fin + LAT)
            if not left[k]:
                cand.setdefault(ops[k]["q"], []).append(k)
    assert len(order) == n
    return order


PLAN = {}


def plan():
    if "ops" not in PLAN:
        PLAN["ops"] = build()
        PLAN["deps"] = depend(PLAN["ops"])
        PLAN["order"] = schedule(PLAN["ops"], PLAN["deps"])
    return PLAN["ops"], PLAN["deps"], PLAN["order"]


def routes(cores, topo):
    out = []
    for c in cores:
        peers = [d for d in cores if d != c and topo.same_plane(c, d)]
        far = [d for d in cores if d != c and not topo.same_plane(c, d)]
        mine = sorted(peers + [c]).index(c)
        hop = {}
        for k, d in enumerate(far):
            own = (mine + k) % 2 == 0
            hop[d] = [h for h in topo.cores_of(c) if h not in cores and topo.may_write(h, d) and (topo.die(h) == topo.die(c)) == own][0]
        out.append((peers, hop))
    return out


def slot(cores, src, dst, topo):
    rest = [c for c in cores if c != dst]
    return sorted(rest, key=lambda c: (not topo.same_plane(c, dst), c)).index(src)


def bits(es):
    return sum(1 << e for e in es)


def onchip(c, peers, topo, h):
    off = topo.engines(c, peers[0])
    return [e for e in topo.engines(c, h) if e not in off]


def hand_on(g, core, T, topo):
    cores = list(T.cores)
    for c, (peers, hop) in zip(cores, routes(cores, topo)):
        for d, h in hop.items():
            if h != core:
                continue
            es, into = topo.engines(core, d), onchip(c, peers, topo, h)
            rid, pid = topo.addr(d, core)
            k = slot(cores, c, d, topo)
            for t in range(2):
                for b in range(NB):
                    g.wait_ge(T.sem["hin%d_%d" % (t, b)], len(into))
                    o = k * W + BW * b
                    g.remote_dma(T["LO%d" % t][:, o:o + BW], T["HB"][:, t * W + BW * b:t * W + BW * b + BW],
                                 T.sem["far%d_%d" % (t, b)], T.sem["hs"], pid, rid, bits(es))
            g.wait_ge(T.sem["hs"], 2 * NB * len(es))


def rank_program(g, core, T, topo):
    if T.rank_of(core) is None:
        hand_on(g, core, T, topo)
        return
    cores = list(T.cores)
    rt = routes(cores, topo)
    peers, hop = rt[T.rank_of(core)]
    ops, deps, order = plan()
    eng = {"v": g.vector, "s": g.scalar, "t": g.tensor, "y": g.sync, "g": g}
    sent = [0]

    def send(g_, T_, t, b):
        p, hs = peers[0], list(hop.values())
        src = T["O%d" % t][:, BW * b:BW * b + BW]
        dst = lambda h: DstId(rid=topo.addr(h, core)[0], pnc=topo.addr(h, core)[1])
        k = slot(cores, core, p, topo) * W + BW * b
        e0, e1 = topo.engines(core, p), onchip(core, peers, topo, hs[0])
        g.remote_dma_fused([
            RemoteDMATransfer(dst_ids=[dst(p)], dma_engine_mask=bits(e0), remote_sem=T.sem["arr%d_%d" % (t, b)],
                              srcs=[src], dsts=[T["LO%d" % t][:, k:k + BW]]),
            RemoteDMATransfer(dst_ids=[dst(h) for h in hs], dma_engine_mask=bits(e1), remote_sem=T.sem["hin%d_%d" % (t, b)],
                              srcs=[src], dsts=[T["HB"][:, t * W + BW * b:t * W + BW * b + BW] for h in hs])],
            local_sem=T.sem["snd"])
        sent[0] += len(e0) + len(e1)

    arrive = {"a": len(topo.engines(peers[0], core)), "f": sum(len(topo.engines(h[core], core)) for _, h in rt if core in h)}
    X = {"send": send}
    cnt = {"v": 0, "s": 0, "t": 0, "g": 0}
    clock = {q: {} for q in eng}
    done = {}
    pos = {i: k for k, i in enumerate(order)}
    nd = 0
    for i in order:
        o = ops[i]
        if o["kind"] == "x":
            n = arrive[o["fn"][0]]
            done[i] = (o["fn"], n, {o["fn"]: n})
            continue
        q = o["q"]
        ck = clock[q]
        for j in sorted(deps[i], key=lambda j: -pos[j]):
            if j in done:
                s, n, c2 = done[j]
                if ck.get(s, 0) < n:
                    eng[q].wait_ge(T.sem[s], n)
                    for k, v in c2.items():
                        ck[k] = max(ck.get(k, 0), v)
        ins = o["fn"](g, T, X)
        if o["kind"] == "c":
            cnt[q] += 1
            s, n = "q" + q, cnt[q]
            ins.then_inc(T.sem[s], 1)
        elif o["kind"] == "d":
            s, n = "d%d" % nd, 16
            nd += 1
            ins.then_inc(T.sem[s], 16)
        else:
            continue
        c2 = dict(ck)
        c2[s] = n
        done[i] = (s, n, c2)
    for q, n in cnt.items():
        g.wait_ge(T.sem["q" + q], n)
    for k in range(nd):
        g.wait_ge(T.sem["d%d" % k], 16)
    g.wait_ge(T.sem["snd"], sent[0])
